import numpy as np, ml_dtypes
CORES = [40,64,80,88,96,104,120,144]
N = 8
import mx_ref
BF = ml_dtypes.bfloat16
def gentries(a):
    return np.ascontiguousarray(a.reshape(8, 16, -1).transpose(0, 2, 1)).reshape(8, -1)
def gtable(e):
    e = np.asarray(e); return np.ascontiguousarray(e.reshape(8, -1, 16).transpose(0, 2, 1)).reshape(128, -1).astype(np.int32)
def gcols(t, e):
    v = np.concatenate([t.reshape(8, 16, -1, 4), np.zeros((8, 16, 1, 4), BF)], axis=2)
    return np.ascontiguousarray(np.stack([v[g][:, e[g]] for g in range(8)])).reshape(128, -1)
def tile(rs):
    return np.stack(rs, axis=2).reshape(128, -1).astype(BF)
def cut(t, i, w=512):
    return t[:, w * i:w * i + w]
def pick(q, e):
    c = np.concatenate([q[0].reshape(128, -1, 4), np.zeros((128, 1, 4), np.uint8)], axis=1); s = np.concatenate([q[1], np.ones((16, 1), np.uint8)], axis=1)
    return (np.ascontiguousarray(c[:, e].reshape(128, -1)), np.ascontiguousarray(s[:, e]))
def join(*qs):
    return (np.concatenate([q[0] for q in qs], axis=1), np.concatenate([q[1] for q in qs], axis=1))
def put(q, e, v):
    c, s = q[0].reshape(128, -1, 4).copy(), q[1].copy(); c[:, e] = v[0].reshape(128, -1, 4); s[:, e] = v[1]
    return (c.reshape(128, -1), s)
def pk(c, s):
    return (np.ascontiguousarray(c), mx_ref.live(s))
def emit(q):
    return q[0], q[1]
def packed(v, rng):
    q = [mx_ref.quantize(np.ascontiguousarray(v[r])) for r in range(N)]
    return np.stack([a for a, b in q]), np.stack([mx_ref.plane(b, rng) for a, b in q])
def values_of_codes():
    e, c = np.zeros((128, 128, 4), np.float32), np.zeros((128, 2, 4), np.uint8)
    e[np.arange(128), np.arange(128), 0] = 1
    c[:127, :, 0] = np.arange(256).reshape(2, 128).T[:127]
    return mx_ref.matmul(mx_ref.quantize(e.reshape(128, 512).astype(BF)), (c.reshape(128, 8), np.full((16, 2), 127, np.uint8))).T.reshape(-1).astype(np.float64)
CODE_VALUE, SCALE_VALUE = values_of_codes(), 2.0 ** (np.arange(256) - 127.0)
def decode(q):
    return (CODE_VALUE[q[0]].reshape(16, 8, -1, 4) * SCALE_VALUE[q[1]][:, None, :, None] + 0.0).reshape(128, -1).astype(np.float32)
def f(rng, *shape):
    return mx_ref.flush((rng.standard_normal(shape, dtype=np.float32) * np.exp2(rng.integers(-2, 3, shape[:-1] + (1,)))).astype(BF))
def wide(rng, *shape, cols=0):
    v = rng.standard_normal(shape, dtype=np.float32) * np.exp2(rng.integers(-12, 13, shape)).astype(np.float32)
    if cols: v *= np.repeat(np.exp2(rng.integers(-cols, cols + 1, shape[:-2] + (1, shape[-1] // 4))) * (rng.random(shape[:-2] + (1, shape[-1] // 4)) > 0.0625), 4, axis=-1).astype(np.float32)
    return mx_ref.flush(v.astype(BF))
C, G, R, L = 384, 192, 3, 3
def big(v, k):
    v = v.astype(np.float32) * np.float32(k)
    v[np.abs(v) < np.float32(2.0 ** -16)] = 0
    return v.astype(BF)
def numbers_of(rng):
    return {"x": big(f(rng, N, 128, 4 * C), 1), "gh": big(f(rng, N, 128, 4 * G), 1), "u": np.array(f(rng, N, 128, 512)), "v": np.array(f(rng, N, 128, 512))}
def weights(rng, w):
    c, p = packed(np.stack([w] * N), rng)
    return {"wc": c, "ws": p}
def still(rng):
    w = np.zeros((128, 4, 128, 4), np.float32)
    i = np.arange(128)
    for b in range(4): w[i, b, i, b] = 32
    return weights(rng, w.reshape(128, 2048).astype(BF))
def matching(rng, n):
    p, i = np.arange(C), rng.permutation(C)[:n]
    h = n // 2
    p[i[:h]] = i[h:2 * h]
    p[i[h:2 * h]] = i[:h]
    return p
def stored(nx, pr):
    return {"nx": np.stack([gtable(nx[r]) for r in range(N)]), "pr": np.stack([gtable(pr[r].reshape(8, R * C)) for r in range(N)])}
def lists_of(rng, same=(), halves=()):
    nx = rng.permuted(np.tile(np.arange(C + G), (N, 8, 1)), axis=2)
    for r in same: nx[r] = nx[r, 0].copy()
    pr = np.stack([matching(rng, C) for i in range(N * 8 * R)]).reshape(N, 8, R, C)
    h = C // 2
    for r in halves:
        for g in range(8):
            for lo, hi in ((0, h), (h, C), (C, C + G)): nx[r, g, lo:hi] = lo + rng.permutation(hi - lo)
            i = h + rng.permutation(h)
            pr[r, g, 0, :h] = i
            pr[r, g, 0, i] = np.arange(h)
    return stored(nx, pr)
def signs(rng):
    return np.stack([rng.permutation(8) % 2 * 2.0 - 1.0 for r in range(N)])
def linked(rng, kind):
    i, a, b, n = rng.permutation(C + G), rng.permutation(C), C + rng.permutation(G), np.arange(C + G)
    if kind == 1: n[i] = np.roll(i, -1)
    if kind == 2:
        n[a] = np.roll(a, -1)
        n[b] = np.roll(b, -1)
    if kind == 3:
        i = np.concatenate([np.stack([a[:G], b], axis=1).reshape(-1), a[G:]])
        n[i] = np.roll(i, -1)
    if kind == 4:
        n[i[::2]] = i[1::2]
        n[i[1::2]] = i[::2]
    if kind == 5: n = np.roll(n, -1)
    if kind == 6: n = np.roll(n, 1)
    if kind == 7: n = i
    return n
def setup_inputs(rng):
    return {**numbers_of(rng), **lists_of(rng), **weights(rng, f(rng, 128, 2048))}
def setup_inputs_ties(rng):
    d = numbers_of(rng)
    c = big(f(rng, 128, 4), 1).astype(np.float32).reshape(8, 16, 4)[:, :8]
    k = np.stack([rng.permutation(C + G) % 2 for r in range(N)])
    k[rng.integers(N)] = 1
    a = np.where(k[:, None, None, :, None] == 1, c[None, :, :, None, :], np.float32(0.0)).astype(BF)
    d["x"].reshape(N, 8, 16, C, 4)[:, :, :8] = a[:, :, :, :C]
    d["gh"].reshape(N, 8, 16, G, 4)[:, :, :8] = a[:, :, :, C:]
    keep = np.zeros((8, 16, 8), bool)
    for g in range(8): keep[g, :8, g] = True
    u = d["u"].reshape(N, 8, 16, 128, 4)
    a = u[:, :, :, ::16].astype(np.float32)
    a[:, ~keep] = 0
    u[:, :, :, ::16] = a.astype(BF)
    w = np.array(f(rng, 128, 2048)).reshape(8, 16, 4, 8, 16, 4)
    w[:, 8:, :, :, :8] = 0
    for g in range(8):
        for h in range(8):
            if g != h: w[h, :, :, g, :8] = 0
    return {**d, **lists_of(rng), **weights(rng, w.reshape(128, 2048))}
def setup_inputs_near(rng):
    d = numbers_of(rng)
    m = np.stack([rng.permutation(8) + 1 for r in range(N)])
    s = rng.integers(0, 2 ** m[:, :, None], (N, 8, C + G))
    sg, o = signs(rng), rng.permutation(N)
    full = int(np.flatnonzero(o == 3)[0])
    h = 2 ** (m[full][:, None] - 1)
    s[full] = s[full] % h + h * ((np.arange(C + G) >= C // 2)[None, :] == (sg[full] > 0)[:, None])
    g = ((s[..., None] >> np.arange(8)) & 1) * np.exp2(np.arange(8) - 23.0)
    a = np.abs(np.concatenate([d["x"], d["gh"]], axis=2).astype(np.float32)).reshape(N, 8, 16, C + G, 4)
    a[:, :, 0] = 0
    a[:, :, 0, :, 0] = 0.5
    a[:, :, 8] = g[..., :4]
    a[:, :, 9] = g[..., 4:]
    a[:, :, 10:] = rng.integers(4, 8, (N, 8, 6, C + G, 4)) * 2.0 ** -20
    a = (a * np.float32(2.0 ** -7)).reshape(N, 128, 4 * (C + G)).astype(BF)
    k = sg * np.exp2(np.array([-30.0, 0.0, 24.0])[o % 3])[:, None]
    u = d["u"].reshape(N, 128, 128, 4)
    u[:, :, ::16] = 0
    for h in range(8):
        z = k[:, h].astype(np.float32).astype(BF)
        u[:, 16 * h, 16 * h, 0] = z
        u[:, 16 * h + 8:16 * h + 10, 16 * h] = z[:, None, None]
    return {**d, "x": np.ascontiguousarray(a[:, :, :4 * C]), "gh": np.ascontiguousarray(a[:, :, 4 * C:]), **lists_of(rng, (), (full,)), **still(rng)}
def setup_inputs_huge(rng):
    d = numbers_of(rng)
    a = 2.0 ** 29 * (0.6 + 0.4 * rng.random((N, 128, C + G, 4)))
    c = np.stack([rng.permutation(C + G) % 2 * 2.0 - 1.0 for r in range(N)])
    one = rng.permutation(N) < N // 2
    c[one] = 1
    a = (a * c[:, None, :, None]).astype(np.float32).reshape(N, 128, 4 * (C + G)).astype(BF)
    z = 2.0 ** 30 * (1 - 0.25 * rng.random((N, 128, 8, 4))) * signs(rng)[:, None, :, None]
    d["u"].reshape(N, 128, 128, 4)[:, :, ::16] = z.astype(np.float32).astype(BF)
    return {**d, "x": np.ascontiguousarray(a[:, :, :4 * C]), "gh": np.ascontiguousarray(a[:, :, 4 * C:]), **lists_of(rng, np.flatnonzero(~one)), **still(rng)}
def setup_inputs_shapes(rng):
    e = rng.permutation(N)
    kinds = np.stack([rng.permutation(8) for r in range(N)])
    kinds[e[0]] = 2
    kinds[e[1]] = 3
    nx = np.stack([linked(rng, kinds[r, g]) for r in range(N) for g in range(8)]).reshape(N, 8, C + G)
    j = np.arange(C)
    pr = np.zeros((N, 8, R, C), int)
    for r in range(N):
        o = rng.permutation(8)
        for g in range(8):
            for t in range(R): pr[r, g, t] = (j, j ^ 1, C - 1 - j, matching(rng, C // 2))[(o[g] + t) % 4]
    return {**numbers_of(rng), **stored(nx, pr), **weights(rng, f(rng, 128, 2048))}
def setup_inputs_spread(rng):
    d = setup_inputs(rng)
    d["x"] = big(wide(rng, N, 128, 4 * C, cols=6), 1)
    d["gh"] = big(wide(rng, N, 128, 4 * G, cols=6), 1)
    return d
def check_inputs(d):
    b = []
    for k in ("x", "gh", "u", "v"):
        a = np.abs(d[k].astype(np.float32))
        if not (np.isfinite(a).all() and ((a == 0) | (a >= 2.0 ** -30) & (a <= 2.0 ** 30)).all()): b.append("a value of " + k)
    for r in range(N):
        if (np.sort(gentries(d["nx"][r]), axis=1) != np.arange(C + G)).any(): b.append("nx of rank %d is no permutation in some group" % r)
        p = gentries(d["pr"][r]).reshape(8, R, C)
        if (p < 0).any() or (p >= C).any(): b.append("pr of rank %d out of range" % r)
        elif (np.take_along_axis(p, p, axis=2) != np.arange(C)).any(): b.append("pr of rank %d: a partner's partner is another column" % r)
    if (d["wc"] != d["wc"][:1]).any(): b.append("wc differs between ranks")
    s = [mx_ref.live(p) for p in d["ws"]]
    if any((p != s[0]).any() for p in s): b.append("ws differs between ranks")
    return b
def read(X, n):
    p = np.argsort(n, axis=1)
    return (gcols(X, n[:, :C]).astype(np.float32) + gcols(X, p[:, :C]).astype(np.float32)).astype(BF)
def reference(x, gh, u, v, nx, pr, wc, ws):
    w = pk(wc[0], ws[0])
    layer = [pick(w, np.arange(128 * b, 128 * b + 128)) for b in range(4)]
    qu = [mx_ref.quantize(u[r]) for r in range(N)]
    now = [np.concatenate([x[r], gh[r]], axis=1) for r in range(N)]
    link = [gentries(nx[r]) for r in range(N)]
    pair = [gentries(pr[r]).reshape(8, R, C) for r in range(N)]
    j = np.arange(C)
    for t in range(R):
        made = []
        for r in range(N):
            q = mx_ref.quantize(read(now[r], link[r]))
            s = mx_ref.matmul(qu[r], q)[::16] + np.float32(0.0)
            a, n = pair[r][:, t], link[r][:, :C]
            o = np.take_along_axis(s, a, axis=1)
            swap = (j < a) & (s < o) | (j > a) & (o < s)
            link[r] = np.concatenate([np.where(swap, np.take_along_axis(n, a, axis=1), n), link[r][:, C:]], axis=1)
            h = tile([np.maximum(mx_ref.matmul(layer[b], q), np.float32(0.0)) * np.float32(0.015625) for b in range(4)])
            made.append(decode(mx_ref.quantize(h)).astype(BF))
        for r in range(N):
            now[r] = np.concatenate([made[r], cut(made[r ^ (1 << t % L)], 0, 4 * G)], axis=1)
    y, nl = np.zeros((N, 128, C), np.float32), np.zeros((N, 8, C + G), np.float32)
    oc, osc = np.zeros((N, 128, 4 * C), np.uint8), np.zeros((N, 16, C), np.uint8)
    for r in range(N):
        q = mx_ref.quantize(read(now[r], link[r]))
        y[r] = mx_ref.matmul(mx_ref.quantize(v[r]), q)
        nl[r] = link[r]
        oc[r], osc[r] = emit(q)
    return {"y": y, "nl": nl, "oc": oc, "osc": osc}

@@ -1,0 +1,426 @@
+from concourse.bass import DstId, RemoteDMATransfer
+from concourse.mybir import dt, AluOpType, ActivationFunctionType
+
+C, G, R, WIN = 384, 192, 3, 576
+H = G
+STEP, KILL = 800, 16383
+F8, BF, F32, I32, U16, U8 = "float8_e4m3fn_x4", "bfloat16", "float32", "int32", "uint16", "uint8"
+CY, GATHER, SCATTER, WAKE, HOPS, FIRST = 0.0011, 1.5, 3.6, 0.1, 5.0, 3.0
+ON_VECTOR = (106, 130, 134, 144, 150, 152, 165, 228, 234, 236, 238, 249, 251, 270, 293, 302, 312, 320, 322, 324)
+ORDER = [int(k) for k in """
+11 8 20 12 21 26 22 9 27 28 10 0 36 5 2 6 1 7 17 14 4 38 3 15 42 325 41 37 67 18 24 16 69 43 39 40 73 71 45 89 87 44 47 46 68 70
+74 72 75 76 77 80 81 78 79 88 50 82 83 23 93 56 62 84 91 90 94 13 63 65 19 48 64 101 92 57 29 95 104 126 122 96 52 51 102 103 120
+105 53 106 107 113 30 124 127 31 33 123 125 34 85 86 133 54 35 135 131 32 129 114 108 121 55 97 115 25 98 116 117 128 139 132 141
+49 109 134 130 143 110 137 118 136 142 58 99 100 111 145 119 147 112 149 144 138 140 146 151 150 152 148 155 156 153 154 157 159
+158 160 161 162 173 174 175 176 179 164 165 66 163 177 168 169 166 167 59 182 187 180 170 215 216 171 178 181 172 188 189 221 217
+218 183 184 190 219 220 212 210 191 192 60 185 211 206 207 193 199 213 208 209 214 225 223 227 194 200 201 222 202 186 195 196 197
+203 198 204 226 224 229 231 233 237 228 205 235 232 234 230 238 236 239 240 241 243 242 244 245 246 247 252 248 261 262 250 259 263
+260 251 61 253 249 254 255 273 256 303 307 305 265 264 266 301 274 268 275 267 306 276 269 304 277 278 270 271 292 293 257 258 298
+299 308 296 297 279 294 285 295 280 286 300 287 309 272 288 281 310 302 311 289 326 282 312 283 284 290 291 315 316 313 314 317 318
+319 320 321 322 323 324 327 328 329 330 331 332 333 334 346 347 344 340 335 337 342 345 336 343 338 339 341 348 349 356 351 354 353
+350 355 352 357""".split()]
+
+SCRATCH = {n: ("sbuf", [128, w], d) for n, w, d in (
+    ("nxi", 36, I32), ("pri", 72, I32), ("xw", 4 * WIN, BF), ("ut", 512, BF), ("vt", 512, BF), ("wq", 512, F8), ("wsc", 512, U8),
+    ("J", WIN, F32), ("J2", C, F32), ("half", WIN, F32), ("pi", 1, I32), ("qi", 1, I32), ("qf", 1, F32), ("qk", 1, F32), ("kq", 1, F32), ("nkq", 1, F32),
+    ("kk", 1, F32), ("e4", 1, F32), ("t4", 4, F32), ("kq4", 4, F32),
+    ("jm", C, F32), ("cc", C, F32), ("ccb", C, BF), ("jo", 72, F32), ("joq", 72, F32), ("uo", 8, I32), ("uof", 8, U16),
+    ("ab", 528, BF), ("ee", 528, BF), ("eq", 512, F8), ("es", 512, U8),
+    ("uq", 128, F8), ("us", 128, U8), ("uq16", 128, F8), ("us16", 128, U8), ("vq", 128, F8), ("vs", 128, U8),
+    ("nxo", 36, U16), ("nx4", 96, U16), ("pv4", 96, U16), ("pvo", 96, U16), ("nxl", 96, U16), ("pro", 72, U16), ("so", 72, U16),
+    ("prf", 72, F32), ("dpr", 72, F32), ("kd", 72, F32), ("base", 72, F32), ("ta", 72, F32), ("tb", 72, F32),
+    ("dn", 72, F32), ("dk", 72, F32), ("db", 72, F32), ("pa", 72, F32), ("pf", 96, F32),
+    ("nxr", WIN + 3 * C, F32), ("pvr", WIN, F32), ("df", 3 * WIN, F32), ("D", 3 * C, F32), ("T1", C, F32), ("NT1", C, F32),
+    ("sw", WIN, BF), ("swp", C, BF), ("scq", C, BF), ("scs", C, BF), ("scn", C, F32), ("scp", C, F32), ("dnr", C, F32), ("scd", C, F32), ("y_sb", C, F32))}
+for _t in range(R + 1):
+    SCRATCH.update({"%s%d" % (n, _t): ("sbuf", [128, w], d) for n, w, d in (("P", 4 * C, BF), ("z", 4 * C, BF), ("zq", C, F8), ("zs", C, U8))})
+    if _t < R:
+        SCRATCH["win%d" % (_t + 1)] = ("sbuf", [128, 4 * WIN], BF)
+        SCRATCH.update({"%s%d" % (n, _t): ("sbuf", [128, w], d) for n, w, d in (
+            ("h", 4 * C, BF), ("hq", C, F8), ("hs", C, U8), ("rc", G // 2, F8), ("rs", G, U8), ("gq", G, F8), ("gs", G, U8))})
+for _b in range(8):
+    SCRATCH["pb%d" % _b] = ("psum", [128, 512], F32)
+
+SEMAPHORES = (["c%d" % i for i in range(60)] + ["d%d" % i for i in range(30)]
+              + ["rarr%d" % t for t in range(R)] + ["garr%d" % t for t in range(R)] + ["sent"])
+
+
+def mask_of(engines):
+    m = 0
+    for e in engines:
+        m |= 1 << e
+    return m
+
+
+def relays_of(core, dest, topo):
+    c = [k for k in topo.cores_of(core) if k != core and topo.may_write(k, dest)]
+    near = [k for k in c if topo.die(k) == topo.die(core)]
+    far = [k for k in c if topo.die(k) != topo.die(core)]
+    return [near[0], far[0], near[1]]
+
+
+def hop_engines(core, relays, topo):
+    e0, e1, e2 = (topo.engines(core, k) for k in relays)
+    h = len(e0) // 2
+    return [e0[:h], e1[h:], e2]
+
+
+def relay_program(g, core, T, topo):
+    mine = [c for c in T.cores if c in topo.cores_of(core)]
+    if not mine:
+        return
+    src = mine[0]
+    r = T.rank_of(src)
+    total = 0
+    for t in range(R):
+        dest = T.cores[r ^ (1 << t)]
+        rel = relays_of(src, dest, topo)
+        if core not in rel:
+            continue
+        k = rel.index(core)
+        rid, pid = topo.addr(dest, core)
+        if k < 2:
+            a, b = k * (G // 2), (k + 1) * (G // 2)
+            out, inn = T["gq%d" % t][:, a:b].bitcast(dt.uint8), T["rc%d" % t][:, :].bitcast(dt.uint8)
+        else:
+            out, inn = T["gs%d" % t][:, :], T["rs%d" % t][:, :]
+        g.wait_ge(T.sem["rarr%d" % t], len(hop_engines(src, rel, topo)[k]))
+        g.remote_dma(out, inn, T.sem["garr%d" % t], T.sem["sent"], pid, rid, topo.mask(core, dest))
+        total += len(topo.engines(core, dest))
+    if total:
+        g.wait_ge(T.sem["sent"], total)
+
+
+def dependencies(ops):
+    hist, out = {}, []
+    for i, o in enumerate(ops):
+        deps = set(o.get("after", ()))
+        for k, lo, hi in o["r"]:
+            deps |= {j for (a, b, j, wr) in hist.get(k, ()) if wr and a < hi and lo < b}
+        for k, lo, hi in o["w"]:
+            deps |= {j for (a, b, j, wr) in hist.get(k, ()) if a < hi and lo < b}
+        for k, lo, hi in o["w"]:
+            lst = hist.setdefault(k, [])
+            lst[:] = [e for e in lst if not (lo <= e[0] and e[1] <= hi)]
+            lst.append((lo, hi, i, True))
+        for k, lo, hi in o["r"]:
+            hist.setdefault(k, []).append((lo, hi, i, False))
+        deps.discard(i)
+        out.append(deps)
+    return out
+
+
+def arrange(ops):
+    at = {k: i for i, k in enumerate(ORDER)}
+    assert sorted(at) == list(range(len(ops)))
+    assert all(at[j] < at[i] for i, d in enumerate(dependencies(ops)) for j in d)
+    assert all(ops[i]["q"] == "vs" for i in ON_VECTOR)
+    readers = {}
+    for i, o in enumerate(ops):
+        if o["q"] == "vs":
+            o["q"] = "v" if i in ON_VECTOR else "s"
+        for k, lo, hi in o["r"]:
+            if k[0] == "@":
+                readers.setdefault(k, set()).add(i)
+    free, names = ["pb%d" % b for b in range(8)], {}
+    for i in ORDER:
+        o = ops[i]
+        if "m" in o:
+            names[o["w"][0][0]] = o["m"]["k"] = free.pop(0)
+        for k, lo, hi in o["r"]:
+            if k[0] == "@":
+                readers[k].discard(i)
+                if not readers[k]:
+                    free.append(names[k])
+    for o in ops:
+        o["after"] = ()
+        for a in "rw":
+            o[a] = [(names.get(k, k), lo, hi) for k, lo, hi in o[a]]
+    return [ops[i] for i in ORDER]
+
+
+def emit(g, T, ops):
+    queues = {"g": g, "v": g.vector, "s": g.scalar, "p": g.tensor, "y": g.sync}
+    know, at, need, used = {q: set() for q in queues}, [], [], set()
+    for i, (o, deps) in enumerate(zip(ops, dependencies(ops))):
+        w = []
+        if o["q"] is None:
+            at.append(set())
+        else:
+            kq = know[o["q"]]
+            for j in sorted(deps, reverse=True):
+                if j not in kq:
+                    w.append(j)
+                    used.add(j)
+                    kq.add(j)
+                    kq |= at[j]
+            at.append(set(kq))
+        need.append(w)
+    last, count, sem = {}, {}, {}
+    for i, o in enumerate(ops):
+        if i not in used:
+            continue
+        if o["q"] is None:
+            sem[i] = (o["sem"], o["val"])
+            continue
+        kind, n = ("d", 16) if o.get("dma") else ("c", 1)
+        k = 0
+        while (kind, k) in last and last[(kind, k)] not in at[i]:
+            k += 1
+        last[(kind, k)] = i
+        count[(kind, k)] = count.get((kind, k), 0) + n
+        sem[i] = ("%s%d" % (kind, k), count[(kind, k)])
+    for i, o in enumerate(ops):
+        if o["q"] is None:
+            continue
+        e = queues[o["q"]]
+        for j in need[i]:
+            e.wait_ge(T.sem[sem[j][0]], sem[j][1])
+        if o["f"] is None:
+            continue
+        ins = o["f"](e, o["q"])
+        if i in sem:
+            ins.then_inc(T.sem[sem[i][0]], 16 if o.get("dma") else 1)
+
+
+def rank_program(g, core, T, topo):
+    rank = T.rank_of(core)
+    if rank is None:
+        return relay_program(g, core, T, topo)
+    ops = []
+    ADD, SUB, MUL, MAX, MIN = AluOpType.add, AluOpType.subtract, AluOpType.mult, AluOpType.max, AluOpType.min
+    LT, AND = AluOpType.is_lt, AluOpType.bitwise_and
+    ACT = ActivationFunctionType
+
+    def op(q, f, r, w, c, **kw):
+        ops.append(dict(q=q, f=f, r=list(r), w=list(w), c=c, **kw))
+        return len(ops) - 1
+
+    def full(*names):
+        return [(n, 0, 1 << 20) for n in names]
+
+    def el(n):
+        return 0.02 + max(64, n) * CY
+
+    def move(out, src, r, w, lat=2.0, q="y"):
+        op(q, lambda e, q: e.dma_start(out, src), r, w, 0.06, dma=True, lat=lat)
+
+    def copy(out, in_, r, w, n, q="vs", scale=None):
+        def f(e, q):
+            if q == "v":
+                return e.tensor_copy(out(), in_()) if scale is None else e.tensor_scalar(out(), in_(), scale, None, MUL)
+            return e.activation(out(), in_(), ACT.Copy) if scale is None else e.activation(out(), in_(), ACT.Copy, scale=scale)
+        op(q, f, r, w, el(n))
+
+    def gather(out, win, off, r, w, n, q="vs"):
+        op(q, lambda e, q: e.tensor_copy(out, win.indirect(off)) if q == "v" else e.activation(out, win.indirect(off), ACT.Copy), r, w, 0.06 + n * GATHER * CY)
+
+    def tt(out, a, b, o, r, w, c):
+        op("v", lambda e, q: e.tensor_tensor(out, a, b, o), r, w, c)
+
+    def ts(out, a, s1, s2, o1, o2, r, w, n=64):
+        if o2 is None:
+            op("v", lambda e, q: e.tensor_scalar(out, a, s1, None, o1), r, w, el(n))
+        else:
+            op("v", lambda e, q: e.tensor_scalar(out, a, s1, s2, o1, o2), r, w, el(n))
+
+    def minus(out, a, col, neg, r, w, n=64):
+        op("vs", lambda e, q: e.tensor_scalar(out, a, T[col][:, 0:1], None, SUB) if q == "v" else
+           e.activation(out, a, ACT.Identity, bias=T[neg][:, 0:1]), r + full(col, neg), w, el(n))
+
+    def times(out, a, col, r, w, n=64):
+        op("vs", lambda e, q: e.tensor_scalar(out, a, T[col][:, 0:1], None, MUL) if q == "v" else
+           e.activation(out, a, ACT.Identity, scale=T[col][:, 0:1]), r + full(col), w, el(n))
+
+    def iota(out, pat, base, cm, w, n, small=True):
+        if small:
+            op("g", lambda e, q: e.iota(out, pat, base, cm, allow_small_or_imprecise_dtypes=True), (), w, 0.13 + 2 * n * CY)
+        else:
+            op("g", lambda e, q: e.iota(out, pat, base, cm), (), w, 0.13 + 2 * n * CY)
+
+    def quant(qn, sn, a, b, src, lo, hi, r):
+        op("v", lambda e, q: e.quantize_mx(T[qn][:, a:b], T[sn][:, a:b], T[src][:, lo:hi]), r, [(qn, a, b)], 0.012 + 0.00022 * (hi - lo))
+
+    made = [0]
+
+    def mm(wn, wsn, wa, xn, xsn, a, b):
+        made[0] += 1
+        m = {"key": full("@%d" % made[0])}
+        op("p", lambda e, q: e.matmul_mx(T[m["k"]][:, 0:b - a], T[wn][:, wa:wa + 128], T[wsn][:, wa:wa + 128], T[xn][:, a:b], T[xsn][:, a:b], True, True),
+           [(wn, wa, wa + 128), (wsn + ".load", 0, 1), (xn, a, b)], m["key"], (b - a + 16) * CY, m=m)
+        m["view"] = lambda: T[m["k"]][:, 0:b - a]
+        return m
+
+    def offs(name, i, lo, n):
+        return T[name][:, 24 * i + lo // 16:24 * i + (lo + n) // 16]
+
+    def read(t, lo, n):
+        for b in range(4):
+            if t == 0:
+                win, key, l1, l2, i = T.xw[:], ("xw", 0, 4 * WIN), "nx4", "pv4", b
+            else:
+                win, key, l1, l2, i = T["win%d" % t][:, WIN * b:WIN * b + WIN], ("win%d" % t, WIN * b, WIN * b + WIN), "pvo", "nxl", t
+            P, k = T["P%d" % t][:, C * b + lo:C * b + lo + n], ("P%d" % t, C * b + lo, C * b + lo + n)
+            gather(P, win, offs(l1, i, lo, n), [(l1, i, i + 1), key], [k], n)
+            tt(T["z%d" % t][:, 4 * lo + b:4 * (lo + n):4], win.indirect(offs(l2, i, lo, n)), P, ADD, [(l2, i, i + 1), key, k],
+               [("z%d.%d" % (t, b), lo, lo + n)], 0.05 + n * GATHER * CY)
+        quant("zq%d" % t, "zs%d" % t, lo, lo + n, "z%d" % t, 4 * lo, 4 * (lo + n), [("z%d.%d" % (t, b), lo, lo + n) for b in range(4)])
+
+    def relu(t, b, lo, n, m):
+        out = T["h%d" % t][:, 4 * lo + b:4 * (lo + n):4]
+        op("vs", lambda e, q: e.activation(out, m["view"](), ACT.Relu, scale=0.015625) if q == "s" else
+           e.tensor_scalar(out, m["view"](), 0.0, 0.015625, MAX, MUL), m["key"], [("h%d.%d" % (t, b), lo, lo + n)], el(n))
+
+    def layer(t, lo, n):
+        for b in range(4):
+            relu(t, b, lo, n, mm("wq", "wsc", 128 * b, "zq%d" % t, "zs%d" % t, lo, lo + n))
+        quant("hq%d" % t, "hs%d" % t, lo, lo + n, "h%d" % t, 4 * lo, 4 * (lo + n), [("h%d.%d" % (t, b), lo, lo + n) for b in range(4)])
+
+    def unpack(t, at, qn, sn, lo, n):
+        for b in range(4):
+            m, a = mm("eq", "es", 128 * b, qn, sn, lo, lo + n), WIN * b + at
+            copy(lambda a=a: T["win%d" % t][:, a:a + n], m["view"], m["key"], [("win%d" % t, a, a + n)], n)
+
+    def exchange(t):
+        dest = T.cores[rank ^ (1 << t)]
+        rel = relays_of(core, dest, topo)
+        en = hop_engines(core, rel, topo)
+        ids = [topo.addr(k, core) for k in rel]
+        hq, hs, rc, rs = T["hq%d" % t], T["hs%d" % t], T["rc%d" % t], T["rs%d" % t]
+        h = G // 2
+
+        def f(e, q):
+            e.remote_dma_fused([RemoteDMATransfer(dst_ids=[DstId(rid=ids[k][0], pnc=ids[k][1])], dma_engine_mask=mask_of(en[k]), remote_sem=T.sem["rarr%d" % t],
+                                                  src=hq[:, h * k:h * k + h].bitcast(dt.uint8), dst=rc[:, :].bitcast(dt.uint8)) for k in range(2)], local_sem=T.sem["sent"])
+            return e.remote_dma(rs[:, :], hs[:, 0:G], T.sem["rarr%d" % t], T.sem["sent"], ids[2][1], ids[2][0], mask_of(en[2]))
+        i = op("g", f, [("hq%d" % t, 0, G)], (), 0.6)
+        op(None, None, (), full("gq%d" % t), 0.0, sem="garr%d" % t, val=sum(len(topo.engines(k, core)) for k in relays_of(dest, core, topo)),
+           lat=HOPS + (FIRST if t == 0 else 0.0), after=[i])
+        return sum(len(x) for x in en)
+
+    def scan(dst, src, a, r, cc="cc", n=C):
+        op("v", lambda e, q: e.tensor_tensor_scan(T[dst][:], T[cc][:], T[src][:, a:a + C], 0.0, ADD, MAX), r + full(cc), full(dst), el(n))
+
+    def nxrow(t):
+        return (0, C) if t == 0 else (WIN + C * (t - 1), WIN + C * t)
+
+    def swap_links(t):
+        a, nt = slice(24 * t, 24 * t + 24), slice(24 * t + 24, 24 * t + 48)
+        tiny = el(24)
+
+        def me(*names):
+            return [(n, t, t + 1) for n in names]
+
+        def nxt(*names):
+            return [(n, t + 1, t + 2) for n in names]
+        df = ("df", WIN * t, WIN * t + WIN)
+        gather(T.dnr[:], T.df[:, df[1]:df[2]], T.pvo[:, a], me("pvo") + [df], full("dnr"), C)
+        scan("scd", "dnr", 0, full("dnr"))
+        minus(T.dn[:, a], T.scd[:, 15:C:16], "kq", "nkq", full("scd"), me("dn"))
+        times(T.dk[:, a], T.dn[:, a], "kk", me("dn"), me("dk"))
+        tt(T.db[:, a], T.pf[:, a], T.dk[:, a], SUB, me("pf", "dk"), me("db"), tiny)
+        for lo, n in ((0, H), (H, C - H)):
+            m = mm("uq16", "us16", 0, "zq%d" % t, "zs%d" % t, lo, lo + n)
+            op("v", lambda e, q, m=m, lo=lo, n=n: e.tensor_tensor(T.T1[:, lo:lo + n], m["view"](), T.D[:, C * t + lo:C * t + lo + n], MUL),
+               m["key"] + me("D"), [("T1", lo, lo + n)], el(n))
+            copy(lambda lo=lo, n=n: T.NT1[:, lo:lo + n], lambda lo=lo, n=n: T.T1[:, lo:lo + n], [("T1", lo, lo + n)], [("NT1", lo, lo + n)], n, scale=-1.0)
+        tt(T.sw[:, 0:C], T.T1[:].indirect(T.pro[:, a]), T.NT1[:], LT, full("T1", "NT1", "pro"), [("sw", 0, C)], 0.05 + C * GATHER * CY)
+        gather(T.swp[:], T.sw[:], T.pvo[:, a], me("pvo") + [("sw", 0, WIN)], full("swp"), C)
+        scan("scq", "swp", 0, full("swp"), "ccb", C // 2)
+        tt(T.pa[:, a], T.scq[:, 15:C:16], T.dn[:, a], MUL, full("scq") + me("dn"), me("pa"), tiny)
+        tt(T.pf[:, nt], T.pa[:, a], T.db[:, a], ADD, me("pa", "db"), nxt("pf"), tiny)
+        copy(lambda: T.pvo[:, nt], lambda: T.pf[:, nt], nxt("pf"), nxt("pvo"), 24, "v")
+        scan("scs", "sw", 0, [("sw", 0, C)], "ccb", C // 2)
+        tt(T.ta[:, a], T.scs[:, 15:C:16], T.dpr[:, a], MUL, full("scs", "dpr"), me("ta"), tiny)
+        tt(T.tb[:, a], T.ta[:, a], T.base[:, a], ADD, me("ta") + full("base"), me("tb"), tiny)
+        copy(lambda: T.so[:, a], lambda: T.tb[:, a], me("tb"), me("so"), 24, "v")
+        (u, v), (c, d) = nxrow(t), nxrow(t + 1)
+        gather(T.nxr[:, c:d], T.nxr[:, u:v], T.so[:, a], me("so") + [("nxr", u, v)], [("nxr", c, d)], C)
+        scan("scn", "nxr", c, [("nxr", c, d)])
+        ts(T.nxl[:, nt], T.scn[:, 15:C:16], T.kq[:, 0:1], None, SUB, None, full("scn", "kq"), nxt("nxl"))
+
+    for out, src, key, lat in (
+            (T.nxi[:], T.nx[:], full("nxi"), 2.1), (T.xw[:, 0:4 * C], T.x[:], [("xw", 0, 4 * C)], 3.8), (T.xw[:, 4 * C:4 * WIN], T.gh[:], [("xw", 4 * C, 4 * WIN)], 4.8),
+            (T.pri[:], T.pr[:], full("pri"), 5.2), (T.wq[:].bitcast(dt.uint8), T.wc[:], full("wq"), 6.5), (T.wsc[:], T.ws[:], full("wsc.load"), 7.0),
+            (T.ut[:], T.u[:], full("ut"), 7.8), (T.vt[:], T.v[:], full("vt"), 8.6)):
+        move(out, src, (), key, lat)
+
+    iota(T.pi[:], [[0, 1]], 0, 1, full("pi"), 1, small=False)
+    iota(T.jm[:], [[0, C // 16], [2 * KILL, 16]], 0, 0, full("jm"), C)
+    iota(T.t4[:], [[1, 4]], 0, 0, full("t4"), 4)
+    op("v", lambda e, q: e.memset(T.half[:], 0.5), (), full("half"), el(WIN))
+    op("v", lambda e, q: e.tensor_tensor_scan(T.J[:], T.half[:], T.half[:], -1.0, ADD, ADD), full("half"), full("J"), el(WIN))
+    iota(T.jo[:], [[0, R], [16, 24]], 0, 0, full("jo"), 72)
+    iota(T.uo[:], [[16, 8]], 0, 0, full("uo"), 8, small=False)
+    iota(T.J2[:], [[1, C]], 0, 0, full("J2"), C)
+    iota(T.sw[:, C:WIN], [[0, G]], 0, 0, [("sw", C, WIN)], G)
+    for k in range(R):
+        iota(T.df[:, WIN * k + C:WIN * k + WIN], [[0, G]], 0, 0, [("df", WIN * k + C, WIN * k + WIN)], G)
+    ts(T.qi[:], T.pi[:], 15, None, AND, None, full("pi"), full("qi"))
+    copy(lambda: T.qf[:], lambda: T.qi[:], full("qi"), full("qf"), 1, "v")
+    ts(T.kq[:], T.qf[:], -float(STEP), 15.0 * STEP, MUL, ADD, full("qf"), full("kq"))
+    ts(T.kk[:], T.qf[:], -2.0, 30.0, MUL, ADD, full("qf"), full("kk"))
+    ts(T.kq4[:], T.t4[:], -0.25, T.kq[:, 0:1], MUL, ADD, full("t4", "kq"), full("kq4"))
+    ts(T.nkq[:], T.kq[:], -1.0, None, MUL, None, full("kq"), full("nkq"))
+    ts(T.qk[:], T.qf[:], 2.0 * KILL, float(KILL), MUL, ADD, full("qf"), full("qk"))
+    ts(T.cc[:], T.jm[:], T.qk[:, 0:1], float(STEP), SUB, MIN, full("jm", "qk"), full("cc"), C)
+    copy(lambda: T.ccb[:], lambda: T.cc[:], full("cc"), full("ccb"), C, "s", 2.0 / STEP)
+    ts(T.e4[:], T.pi[:], -4.0, -4.0, MUL, ADD, full("pi"), full("e4"))
+    op("s", lambda e, q: e.activation(T.ab[:], T.J[:, 0:528], ACT.Abs, bias=T.e4[:, 0:1]), full("J", "e4"), full("ab"), el(528))
+    op("s", lambda e, q: e.activation(T.ee[:], T.ab[:], ACT.Relu, bias=1.0, scale=-1.0), full("ab"), full("ee"), el(528))
+    for b in range(4):
+        quant("eq", "es", 128 * b, 128 * b + 128, "ee", 4 - b, 516 - b, full("ee"))
+
+    copy(lambda: T.nxo[:], lambda: T.nxi[:], full("nxi"), full("nxo"), 36, "v")
+    for b in range(4):
+        ts(T.nx4[:, 24 * b:24 * b + 24], T.nxi[:, 0:24], 4.0, float(b), MUL, ADD, full("nxi"), [("nx4", b, b + 1)])
+    op("v", lambda e, q: e.tensor_copy(T.pvr[:].indirect(T.nxo[:]), T.J[:]), full("J", "nxo"), full("pvr"), 0.05 + WIN * SCATTER * CY)
+    gather(T.nxr[:, 0:WIN], T.J[:], T.nxo[:], full("J", "nxo"), [("nxr", 0, WIN)], WIN, "s")
+    scan("scp", "pvr", 0, full("pvr"))
+    for b in range(4):
+        ts(T.pv4[:, 24 * b:24 * b + 24], T.scp[:, 15:C:16], T.kq4[:, b:b + 1], 4.0, SUB, MUL, full("scp", "kq4"), [("pv4", b, b + 1)])
+    ts(T.pvo[:, 0:24], T.scp[:, 15:C:16], T.kq[:, 0:1], None, SUB, None, full("scp", "kq"), [("pvo", 0, 1)])
+    minus(T.pf[:, 0:24], T.scp[:, 15:C:16], "kq", "nkq", full("scp"), [("pf", 0, 1)])
+    copy(lambda: T.pro[:], lambda: T.pri[:], full("pri"), full("pro"), 72, "v")
+    copy(lambda: T.prf[:], lambda: T.pri[:], full("pri"), full("prf"), 72, "v")
+    ts(T.joq[:], T.jo[:], T.qf[:, 0:1], None, ADD, None, full("jo", "qf"), full("joq"), 72)
+    tt(T.dpr[:], T.prf[:], T.joq[:], SUB, full("prf", "joq"), full("dpr"), el(144))
+    times(T.kd[:], T.dpr[:], "kk", full("dpr"), full("kd"), 72)
+    tt(T.base[:], T.joq[:], T.kd[:], SUB, full("joq", "kd"), full("base"), el(144))
+    for i in range(R):
+        d, key = T.df[:, WIN * i:WIN * i + C], [("df", WIN * i, WIN * i + C)]
+        tt(d, T.J[:, 0:C].indirect(T.pro[:, 24 * i:24 * i + 24]), T.J2[:], SUB, full("J", "J2", "pro"), key, 0.05 + C * GATHER * CY)
+        op("s", lambda e, q, i=i, d=d: e.activation(T.D[:, C * i:C * i + C], d, ACT.Sign), key, [("D", i, i + 1)], el(C))
+    quant("uq", "us", 0, 128, "ut", 0, 512, full("ut"))
+    copy(lambda: T.uof[:], lambda: T.uo[:], full("uo"), full("uof"), 8, "v")
+    op("v", lambda e, q: e.tensor_copy(T.uq16[:, 0:128].bitcast(dt.uint32), T.uq[:, 0:128].bitcast(dt.uint32).indirect(T.uof[:, 0:8])),
+       full("uq", "uof"), full("uq16"), 0.05 + 128 * GATHER * CY)
+    gather(T.us16[:, 0:128], T.us[:, 0:128], T.uof[:, 0:8], full("uq", "uof"), full("us16.load"), 128)
+    quant("vq", "vs", 0, 128, "vt", 0, 512, full("vt"))
+
+    sent = 0
+    for t in range(R):
+        read(t, 0, H)
+        layer(t, 0, H)
+        sent += exchange(t)
+        read(t, H, C - H)
+        swap_links(t)
+        layer(t, H, C - H)
+        unpack(t + 1, 0, "hq%d" % t, "hs%d" % t, 0, H)
+        unpack(t + 1, H, "hq%d" % t, "hs%d" % t, H, C - H)
+        unpack(t + 1, C, "gq%d" % t, "gs%d" % t, 0, G)
+    c, d = nxrow(R)
+    move(T.nl[:, C:WIN], T.nxr[0:128:16, C:WIN], [("nxr", C, WIN)], [("nl", C, WIN)])
+    move(T.nl[:, 0:C], T.nxr[0:128:16, c:d], [("nxr", c, d)], [("nl", 0, C)])
+    zq, zs, qn = T["zq%d" % R], T["zs%d" % R], "zq%d" % R
+    for lo, n in ((0, 256), (256, 128)):
+        read(R, lo, n)
+        m = mm("vq", "vs", 0, qn, "zs%d" % R, lo, lo + n)
+        move(T.oc[:, 4 * lo:4 * (lo + n)], zq[:, lo:lo + n].bitcast(dt.uint8), [(qn, lo, lo + n)], [("oc", lo, lo + n)], 2.3)
+        copy(lambda lo=lo, n=n: T.y_sb[:, lo:lo + n], m["view"], m["key"], [("y_sb", lo, lo + n)], n)
+        move(T.y[:, lo:lo + n], T.y_sb[:, lo:lo + n], [("y_sb", lo, lo + n)], [("y", lo, lo + n)], 2.3)
+    for k in range(4):
+        move(T.osc[4 * k:4 * k + 4, :], zs[32 * k:32 * k + 4, :], [(qn, 0, C)], [("osc", k, k + 1)], q="s")
+    op("y", None, [("oc", 0, C), ("y", 0, C), ("osc", 0, 4), ("nl", 0, WIN)], (), 0.0)
+    emit(g, T, arrange(ops))
+    g.wait_ge(T.sem.sent, sent)

@@ -2,47 +2,49 @@ from concourse.bass import DstId, RemoteDMATransfer
 from concourse.mybir import dt, AluOpType, ActivationFunctionType
 
 C, G, R, WIN = 384, 192, 3, 576
-H = G
-STEP, KILL = 800, 16383
-F8, BF, F32, I32, U16, U8 = "float8_e4m3fn_x4", "bfloat16", "float32", "int32", "uint16", "uint8"
-CY, GATHER, SCATTER, WAKE, HOPS, FIRST = 0.0011, 1.5, 3.6, 0.1, 5.0, 3.0
-ON_VECTOR = (106, 130, 134, 144, 150, 152, 165, 228, 234, 236, 238, 249, 251, 270, 293, 302, 312, 320, 322, 324)
+H, A, B = G, 128, 64
+MID = WIN // 2
+S16, K16 = 640, 2048
+F8, BF, F16, F32, I32, U16, U8 = "float8_e4m3fn_x4", "bfloat16", "float16", "float32", "int32", "uint16", "uint8"
+FIRST_PIECES, REST_PIECES, LAST_PIECES, LAST_TILES = (128, 64), (192,), (256, 128), (256, 128)
+ON_VECTOR = (29, 123, 125, 128, 167, 170, 182, 221, 225, 232, 233, 267, 273, 275, 277, 290, 329, 330, 340, 347, 350, 381, 390, 414)
 ORDER = [int(k) for k in """
-11 8 20 12 21 26 22 9 27 28 10 0 36 5 2 6 1 7 17 14 4 38 3 15 42 325 41 37 67 18 24 16 69 43 39 40 73 71 45 89 87 44 47 46 68 70
-74 72 75 76 77 80 81 78 79 88 50 82 83 23 93 56 62 84 91 90 94 13 63 65 19 48 64 101 92 57 29 95 104 126 122 96 52 51 102 103 120
-105 53 106 107 113 30 124 127 31 33 123 125 34 85 86 133 54 35 135 131 32 129 114 108 121 55 97 115 25 98 116 117 128 139 132 141
-49 109 134 130 143 110 137 118 136 142 58 99 100 111 145 119 147 112 149 144 138 140 146 151 150 152 148 155 156 153 154 157 159
-158 160 161 162 173 174 175 176 179 164 165 66 163 177 168 169 166 167 59 182 187 180 170 215 216 171 178 181 172 188 189 221 217
-218 183 184 190 219 220 212 210 191 192 60 185 211 206 207 193 199 213 208 209 214 225 223 227 194 200 201 222 202 186 195 196 197
-203 198 204 226 224 229 231 233 237 228 205 235 232 234 230 238 236 239 240 241 243 242 244 245 246 247 252 248 261 262 250 259 263
-260 251 61 253 249 254 255 273 256 303 307 305 265 264 266 301 274 268 275 267 306 276 269 304 277 278 270 271 292 293 257 258 298
-299 308 296 297 279 294 285 295 280 286 300 287 309 272 288 281 310 302 311 289 326 282 312 283 284 290 291 315 316 313 314 317 318
-319 320 321 322 323 324 327 328 329 330 331 332 333 334 346 347 344 340 335 337 342 345 336 343 338 339 341 348 349 356 351 354 353
-350 355 352 357""".split()]
+0 5 1 2 13 7 59 25 26 28 3 4 6 27 9 10 29 11 31 32 18 8 14 15 16 12 17 33 34 40 41 42 35 30 43 44 39 19 38 36 37 66 64 62 68 70 72
+76 74 47 45 46 48 67 65 63 69 71 109 103 78 81 85 83 79 82 86 84 80 107 77 75 73 58 110 60 89 87 105 90 94 96 92 95 61 97 91 93 101
+20 102 104 108 106 50 111 112 98 51 53 52 23 21 54 24 55 113 114 117 115 118 141 143 137 146 139 152 150 144 138 56 142 140 147 153
+151 116 119 57 120 49 121 22 88 99 100 122 145 148 156 154 158 160 124 388 386 123 131 134 159 161 155 157 149 166 162 168 164 125
+128 132 126 133 129 127 135 167 163 174 169 165 176 172 178 130 136 182 211 170 183 175 171 177 180 184 217 173 179 186 212 181 185
+218 187 193 191 189 188 215 213 190 194 192 197 216 214 198 204 200 202 199 201 205 203 209 195 210 219 220 196 206 387 207 208 221
+225 251 252 222 226 223 227 224 247 258 259 248 249 260 250 261 245 254 246 255 256 257 228 229 230 253 231 239 232 233 266 268 264
+262 236 242 269 263 265 267 234 240 274 237 235 241 238 243 275 244 276 270 272 282 271 290 277 284 291 283 273 278 280 286 323 288
+292 319 285 279 281 287 294 324 289 293 320 299 297 301 295 321 325 298 300 296 302 305 310 312 308 306 309 311 313 307 322 326 317
+303 327 328 304 314 353 315 318 355 359 357 368 366 364 329 362 330 316 354 333 331 334 332 335 336 337 338 356 360 369 358 367 361
+365 363 376 374 372 370 340 339 341 347 377 344 371 373 378 384 380 382 379 350 348 342 351 345 349 343 352 346 375 385 396 390 381
+383 392 391 397 393 394 395 398 404 400 402 406 407 399 405 403 401 409 411 412 389 408 410 413 414 416 419 418 417 415 420""".split()]
 
 SCRATCH = {n: ("sbuf", [128, w], d) for n, w, d in (
-    ("nxi", 36, I32), ("pri", 72, I32), ("xw", 4 * WIN, BF), ("ut", 512, BF), ("vt", 512, BF), ("wq", 512, F8), ("wsc", 512, U8),
-    ("J", WIN, F32), ("J2", C, F32), ("half", WIN, F32), ("pi", 1, I32), ("qi", 1, I32), ("qf", 1, F32), ("qk", 1, F32), ("kq", 1, F32), ("nkq", 1, F32),
-    ("kk", 1, F32), ("e4", 1, F32), ("t4", 4, F32), ("kq4", 4, F32),
-    ("jm", C, F32), ("cc", C, F32), ("ccb", C, BF), ("jo", 72, F32), ("joq", 72, F32), ("uo", 8, I32), ("uof", 8, U16),
+    ("nxi", 36, I32), ("pri", 72, I32), ("win0", 4 * WIN, BF), ("ut", 512, BF), ("vt", 512, BF), ("wq", 512, F8), ("wsc", 512, U8),
+    ("J", WIN, F32), ("e4", 1, F32), ("pi", 1, I32), ("qi", 1, I32), ("qf", 1, F32), ("q1", 1, F32), ("t4", 4, F32), ("kq4", 4, F32),
+    ("k16", 1, F32), ("k16p", 1, F32), ("jm16", H, BF), ("ca", C, F16), ("c16", H, F16),
+    ("jo", 72, F32), ("joq", 72, F32), ("uo", 8, I32), ("uof", 8, U16),
     ("ab", 528, BF), ("ee", 528, BF), ("eq", 512, F8), ("es", 512, U8),
     ("uq", 128, F8), ("us", 128, U8), ("uq16", 128, F8), ("us16", 128, U8), ("vq", 128, F8), ("vs", 128, U8),
-    ("nxo", 36, U16), ("nx4", 96, U16), ("pv4", 96, U16), ("pvo", 96, U16), ("nxl", 96, U16), ("pro", 72, U16), ("so", 72, U16),
-    ("prf", 72, F32), ("dpr", 72, F32), ("kd", 72, F32), ("base", 72, F32), ("ta", 72, F32), ("tb", 72, F32),
-    ("dn", 72, F32), ("dk", 72, F32), ("db", 72, F32), ("pa", 72, F32), ("pf", 96, F32),
-    ("nxr", WIN + 3 * C, F32), ("pvr", WIN, F32), ("df", 3 * WIN, F32), ("D", 3 * C, F32), ("T1", C, F32), ("NT1", C, F32),
-    ("sw", WIN, BF), ("swp", C, BF), ("scq", C, BF), ("scs", C, BF), ("scn", C, F32), ("scp", C, F32), ("dnr", C, F32), ("scd", C, F32), ("y_sb", C, F32))}
+    ("nxo", 36, U16), ("nx4", 96, U16), ("pv4", 96, U16), ("pvo", 96, U16), ("nxl", 96, U16), ("so", 72, U16), ("loo", 72, U16), ("hio", 72, U16),
+    ("dpr", 72, F32), ("kd", 72, F32), ("base", 72, F32), ("lof", 72, F32), ("hif", 72, F32), ("ta", 72, F32), ("tb", 72, F32),
+    ("nxr", WIN + 3 * C, F32), ("pvr", WIN, F32), ("sr", WIN, F32), ("pvh", C, F16), ("S", C, F32), ("SL", C, F32), ("sw", C, F16),
+    ("scn", C, F32), ("scp", C, F32), ("sch", C, F16), ("scs", C, F16), ("y_sb", C, F32))}
 for _t in range(R + 1):
     SCRATCH.update({"%s%d" % (n, _t): ("sbuf", [128, w], d) for n, w, d in (("P", 4 * C, BF), ("z", 4 * C, BF), ("zq", C, F8), ("zs", C, U8))})
     if _t < R:
         SCRATCH["win%d" % (_t + 1)] = ("sbuf", [128, 4 * WIN], BF)
         SCRATCH.update({"%s%d" % (n, _t): ("sbuf", [128, w], d) for n, w, d in (
-            ("h", 4 * C, BF), ("hq", C, F8), ("hs", C, U8), ("rc", G // 2, F8), ("rs", G, U8), ("gq", G, F8), ("gs", G, U8))})
+            ("h", 8 * A, BF), ("hq", 2 * A, F8), ("hs", 2 * A, U8), ("k", 4 * H, BF), ("kq", H, F8), ("ks", H, U8),
+            ("ra", B, F8), ("rb", B, F8), ("rs", 4 * B, U8), ("gq", G, F8), ("gs", G, U8))})
 for _b in range(8):
     SCRATCH["pb%d" % _b] = ("psum", [128, 512], F32)
 
-SEMAPHORES = (["c%d" % i for i in range(60)] + ["d%d" % i for i in range(30)]
-              + ["rarr%d" % t for t in range(R)] + ["garr%d" % t for t in range(R)] + ["sent"])
+SEMAPHORES = (["c%d" % i for i in range(70)] + ["d%d" % i for i in range(30)]
+              + ["%s%d" % (n, t) for n in ("arra", "arrb", "garr") for t in range(R)] + ["sent"])
 
 
 def mask_of(engines):
@@ -54,15 +56,15 @@ def mask_of(engines):
 
 def relays_of(core, dest, topo):
     c = [k for k in topo.cores_of(core) if k != core and topo.may_write(k, dest)]
-    near = [k for k in c if topo.die(k) == topo.die(core)]
-    far = [k for k in c if topo.die(k) != topo.die(core)]
-    return [near[0], far[0], near[1]]
+    return [[k for k in c if topo.die(k) == topo.die(core)][0], [k for k in c if topo.die(k) != topo.die(core)][0]]
 
 
-def hop_engines(core, relays, topo):
-    e0, e1, e2 = (topo.engines(core, k) for k in relays)
-    h = len(e0) // 2
-    return [e0[:h], e1[h:], e2]
+def plan(t, second):
+    return [(0, A, B), (1, None, G)] if second else [(0, 0, A // 2), (1, A // 2, A // 2)]
+
+
+def hop_engines(core, relays, transfers, topo):
+    return [topo.engines(core, relays[k])[i::len(transfers)] for i, (k, lo, n) in enumerate(transfers)]
 
 
 def relay_program(g, core, T, topo):
@@ -75,18 +77,19 @@ def relay_program(g, core, T, topo):
     for t in range(R):
         dest = T.cores[r ^ (1 << t)]
         rel = relays_of(src, dest, topo)
-        if core not in rel:
-            continue
-        k = rel.index(core)
-        rid, pid = topo.addr(dest, core)
-        if k < 2:
-            a, b = k * (G // 2), (k + 1) * (G // 2)
-            out, inn = T["gq%d" % t][:, a:b].bitcast(dt.uint8), T["rc%d" % t][:, :].bitcast(dt.uint8)
-        else:
-            out, inn = T["gs%d" % t][:, :], T["rs%d" % t][:, :]
-        g.wait_ge(T.sem["rarr%d" % t], len(hop_engines(src, rel, topo)[k]))
-        g.remote_dma(out, inn, T.sem["garr%d" % t], T.sem["sent"], pid, rid, topo.mask(core, dest))
-        total += len(topo.engines(core, dest))
+        for second in (False, True):
+            transfers = plan(t, second)
+            for (k, lo, n), en in zip(transfers, hop_engines(src, rel, transfers, topo)):
+                if rel[k] != core:
+                    continue
+                rid, pid = topo.addr(dest, core)
+                if lo is None:
+                    out, inn = T["gs%d" % t][:, 0:n], T["rs%d" % t][:, 0:n]
+                else:
+                    out, inn = T["gq%d" % t][:, lo:lo + n].bitcast(dt.uint8), T[("rb%d" if second else "ra%d") % t][:, 0:n].bitcast(dt.uint8)
+                g.wait_ge(T.sem[("arrb%d" if second else "arra%d") % t], len(en))
+                g.remote_dma(out, inn, T.sem["garr%d" % t], T.sem["sent"], pid, rid, topo.mask(core, dest))
+                total += len(topo.engines(core, dest))
     if total:
         g.wait_ge(T.sem["sent"], total)
 
@@ -111,7 +114,8 @@ def dependencies(ops):
 
 
 def arrange(ops):
-    at = {k: i for i, k in enumerate(ORDER)}
+    order = ORDER or list(range(len(ops)))
+    at = {k: i for i, k in enumerate(order)}
     assert sorted(at) == list(range(len(ops)))
     assert all(at[j] < at[i] for i, d in enumerate(dependencies(ops)) for j in d)
     assert all(ops[i]["q"] == "vs" for i in ON_VECTOR)
@@ -123,7 +127,7 @@ def arrange(ops):
             if k[0] == "@":
                 readers.setdefault(k, set()).add(i)
     free, names = ["pb%d" % b for b in range(8)], {}
-    for i in ORDER:
+    for i in order:
         o = ops[i]
         if "m" in o:
             names[o["w"][0][0]] = o["m"]["k"] = free.pop(0)
@@ -136,7 +140,7 @@ def arrange(ops):
         o["after"] = ()
         for a in "rw":
             o[a] = [(names.get(k, k), lo, hi) for k, lo, hi in o[a]]
-    return [ops[i] for i in ORDER]
+    return [ops[i] for i in order]
 
 
 def emit(g, T, ops):
@@ -163,7 +167,7 @@ def emit(g, T, ops):
         if o["q"] is None:
             sem[i] = (o["sem"], o["val"])
             continue
-        kind, n = ("d", 16) if o.get("dma") else ("c", 1)
+        kind, n = ("d", 16) if o["c"][0] == "dma" else ("c", 1)
         k = 0
         while (kind, k) in last and last[(kind, k)] not in at[i]:
             k += 1
@@ -180,16 +184,13 @@ def emit(g, T, ops):
             continue
         ins = o["f"](e, o["q"])
         if i in sem:
-            ins.then_inc(T.sem[sem[i][0]], 16 if o.get("dma") else 1)
+            ins.then_inc(T.sem[sem[i][0]], 16 if o["c"][0] == "dma" else 1)
 
 
-def rank_program(g, core, T, topo):
-    rank = T.rank_of(core)
-    if rank is None:
-        return relay_program(g, core, T, topo)
+def calls_of(core, rank, T, topo):
     ops = []
     ADD, SUB, MUL, MAX, MIN = AluOpType.add, AluOpType.subtract, AluOpType.mult, AluOpType.max, AluOpType.min
-    LT, AND = AluOpType.is_lt, AluOpType.bitwise_and
+    LT, GT, EQ, AND = AluOpType.is_lt, AluOpType.is_gt, AluOpType.is_equal, AluOpType.bitwise_and
     ACT = ActivationFunctionType
 
     def op(q, f, r, w, c, **kw):
@@ -199,47 +200,44 @@ def rank_program(g, core, T, topo):
     def full(*names):
         return [(n, 0, 1 << 20) for n in names]
 
-    def el(n):
-        return 0.02 + max(64, n) * CY
+    def move(out, src, r, w, size, q="y"):
+        op(q, lambda e, q: e.dma_start(out, src), r, w, ("dma", size))
 
-    def move(out, src, r, w, lat=2.0, q="y"):
-        op(q, lambda e, q: e.dma_start(out, src), r, w, 0.06, dma=True, lat=lat)
+    def copy(out, in_, r, w, n, q="vs"):
+        op(q, lambda e, q: e.tensor_copy(out(), in_()) if q == "v" else e.activation(out(), in_(), ACT.Copy), r, w, ("e", n))
 
-    def copy(out, in_, r, w, n, q="vs", scale=None):
+    def gather(out, win, off, r, w, n, q="vs", bias=None):
         def f(e, q):
-            if q == "v":
-                return e.tensor_copy(out(), in_()) if scale is None else e.tensor_scalar(out(), in_(), scale, None, MUL)
-            return e.activation(out(), in_(), ACT.Copy) if scale is None else e.activation(out(), in_(), ACT.Copy, scale=scale)
-        op(q, f, r, w, el(n))
-
-    def gather(out, win, off, r, w, n, q="vs"):
-        op(q, lambda e, q: e.tensor_copy(out, win.indirect(off)) if q == "v" else e.activation(out, win.indirect(off), ACT.Copy), r, w, 0.06 + n * GATHER * CY)
+            if bias is None:
+                return e.tensor_copy(out, win.indirect(off)) if q == "v" else e.activation(out, win.indirect(off), ACT.Copy)
+            return e.tensor_scalar(out, win.indirect(off), bias, None, ADD) if q == "v" else e.activation(out, win.indirect(off), ACT.Copy, bias=bias)
+        op(q, f, r, w, ("g", n))
 
     def tt(out, a, b, o, r, w, c):
         op("v", lambda e, q: e.tensor_tensor(out, a, b, o), r, w, c)
 
-    def ts(out, a, s1, s2, o1, o2, r, w, n=64):
+    def ts(out, a, s1, s2, o1, o2, r, w, n=64, kind="e"):
         if o2 is None:
-            op("v", lambda e, q: e.tensor_scalar(out, a, s1, None, o1), r, w, el(n))
+            op("v", lambda e, q: e.tensor_scalar(out, a, s1, None, o1), r, w, (kind, n))
         else:
-            op("v", lambda e, q: e.tensor_scalar(out, a, s1, s2, o1, o2), r, w, el(n))
-
-    def minus(out, a, col, neg, r, w, n=64):
-        op("vs", lambda e, q: e.tensor_scalar(out, a, T[col][:, 0:1], None, SUB) if q == "v" else
-           e.activation(out, a, ACT.Identity, bias=T[neg][:, 0:1]), r + full(col, neg), w, el(n))
+            op("v", lambda e, q: e.tensor_scalar(out, a, s1, s2, o1, o2), r, w, (kind, n))
 
     def times(out, a, col, r, w, n=64):
         op("vs", lambda e, q: e.tensor_scalar(out, a, T[col][:, 0:1], None, MUL) if q == "v" else
-           e.activation(out, a, ACT.Identity, scale=T[col][:, 0:1]), r + full(col), w, el(n))
+           e.activation(out, a, ACT.Identity, scale=T[col][:, 0:1]), r + full(col), w, ("e", n))
+
+    def affine(out, a, s, b):
+        op("vs", lambda e, q: e.tensor_scalar(T[out][:], T[a][:], s, b, MUL, ADD) if q == "v" else
+           e.activation(T[out][:], T[a][:], ACT.Copy, scale=s, bias=b), full(a), full(out), ("e", 1))
 
     def iota(out, pat, base, cm, w, n, small=True):
         if small:
-            op("g", lambda e, q: e.iota(out, pat, base, cm, allow_small_or_imprecise_dtypes=True), (), w, 0.13 + 2 * n * CY)
+            op("g", lambda e, q: e.iota(out, pat, base, cm, allow_small_or_imprecise_dtypes=True), (), w, ("iota", n))
         else:
-            op("g", lambda e, q: e.iota(out, pat, base, cm), (), w, 0.13 + 2 * n * CY)
+            op("g", lambda e, q: e.iota(out, pat, base, cm), (), w, ("iota", n))
 
     def quant(qn, sn, a, b, src, lo, hi, r):
-        op("v", lambda e, q: e.quantize_mx(T[qn][:, a:b], T[sn][:, a:b], T[src][:, lo:hi]), r, [(qn, a, b)], 0.012 + 0.00022 * (hi - lo))
+        op("v", lambda e, q: e.quantize_mx(T[qn][:, a:b], T[sn][:, a:b], T[src][:, lo:hi]), r, [(qn, a, b)], ("q", hi - lo))
 
     made = [0]
 
@@ -247,180 +245,202 @@ def rank_program(g, core, T, topo):
         made[0] += 1
         m = {"key": full("@%d" % made[0])}
         op("p", lambda e, q: e.matmul_mx(T[m["k"]][:, 0:b - a], T[wn][:, wa:wa + 128], T[wsn][:, wa:wa + 128], T[xn][:, a:b], T[xsn][:, a:b], True, True),
-           [(wn, wa, wa + 128), (wsn + ".load", 0, 1), (xn, a, b)], m["key"], (b - a + 16) * CY, m=m)
-        m["view"] = lambda: T[m["k"]][:, 0:b - a]
+           [(wn, wa, wa + 128), (wsn + ".load", 0, 1), (xn, a, b)], m["key"], ("mm", b - a), m=m)
+        m["view"] = lambda lo=a, hi=b: T[m["k"]][:, lo - a:hi - a]
         return m
 
-    def offs(name, i, lo, n):
-        return T[name][:, 24 * i + lo // 16:24 * i + (lo + n) // 16]
+    def read(t, lo, pieces):
+        for n in pieces:
+            for b in range(4):
+                if t == 0:
+                    win, l1, l2, i = T.win0[:], "nx4", "pv4", b
+                else:
+                    win, l1, l2, i = T["win%d" % t][:, WIN * b:WIN * b + WIN], "nxl", "pvo", t
+                key, u, v = ("win%d.%d" % (t, b), 0, WIN), 24 * i + lo // 16, 24 * i + (lo + n) // 16
+                P, k = T["P%d" % t][:, C * b + lo:C * b + lo + n], ("P%d" % t, C * b + lo, C * b + lo + n)
+                gather(P, win, T[l1][:, u:v], [key, (l1, u, v)], [k], n)
+                tt(T["z%d" % t][:, 4 * lo + b:4 * (lo + n):4], win.indirect(T[l2][:, u:v]), P, ADD, [key, (l2, u, v), k], [("z%d.%d" % (t, b), lo, lo + n)], ("g", n))
+            lo += n
 
-    def read(t, lo, n):
-        for b in range(4):
-            if t == 0:
-                win, key, l1, l2, i = T.xw[:], ("xw", 0, 4 * WIN), "nx4", "pv4", b
-            else:
-                win, key, l1, l2, i = T["win%d" % t][:, WIN * b:WIN * b + WIN], ("win%d" % t, WIN * b, WIN * b + WIN), "pvo", "nxl", t
-            P, k = T["P%d" % t][:, C * b + lo:C * b + lo + n], ("P%d" % t, C * b + lo, C * b + lo + n)
-            gather(P, win, offs(l1, i, lo, n), [(l1, i, i + 1), key], [k], n)
-            tt(T["z%d" % t][:, 4 * lo + b:4 * (lo + n):4], win.indirect(offs(l2, i, lo, n)), P, ADD, [(l2, i, i + 1), key, k],
-               [("z%d.%d" % (t, b), lo, lo + n)], 0.05 + n * GATHER * CY)
+    def quant_z(t, lo, n):
         quant("zq%d" % t, "zs%d" % t, lo, lo + n, "z%d" % t, 4 * lo, 4 * (lo + n), [("z%d.%d" % (t, b), lo, lo + n) for b in range(4)])
 
-    def relu(t, b, lo, n, m):
-        out = T["h%d" % t][:, 4 * lo + b:4 * (lo + n):4]
-        op("vs", lambda e, q: e.activation(out, m["view"](), ACT.Relu, scale=0.015625) if q == "s" else
-           e.tensor_scalar(out, m["view"](), 0.0, 0.015625, MAX, MUL), m["key"], [("h%d.%d" % (t, b), lo, lo + n)], el(n))
-
-    def layer(t, lo, n):
+    def layer(t, za, zb, lo, n, hn, at, wide):
+        h = "%s%d" % (hn, t)
         for b in range(4):
-            relu(t, b, lo, n, mm("wq", "wsc", 128 * b, "zq%d" % t, "zs%d" % t, lo, lo + n))
-        quant("hq%d" % t, "hs%d" % t, lo, lo + n, "h%d" % t, 4 * lo, 4 * (lo + n), [("h%d.%d" % (t, b), lo, lo + n) for b in range(4)])
+            m, out = mm("wq", "wsc", 128 * b, "zq%d" % t, "zs%d" % t, za, zb), T[h][:, 4 * at + b:4 * (at + n):4]
+            op("vs", lambda e, q, m=m, out=out: e.activation(out, m["view"](lo, lo + n), ACT.Relu, scale=0.015625) if q == "s" else
+               e.tensor_scalar(out, m["view"](lo, lo + n), 0.0, 0.015625, MAX, MUL), m["key"], [("%s.%d" % (h, b), at, at + n)], ("e", n))
+        quant("%sq%d" % (hn, t), "%ss%d" % (hn, t), at, at + wide, h, 4 * at, 4 * (at + wide), [("%s.%d" % (h, b), at, at + wide) for b in range(4)])
 
-    def unpack(t, at, qn, sn, lo, n):
+    def unpack(t, at, qn, sn, n):
         for b in range(4):
-            m, a = mm("eq", "es", 128 * b, qn, sn, lo, lo + n), WIN * b + at
-            copy(lambda a=a: T["win%d" % t][:, a:a + n], m["view"], m["key"], [("win%d" % t, a, a + n)], n)
+            m = mm("eq", "es", 128 * b, qn, sn, 0, n)
+            copy(lambda b=b: T["win%d" % t][:, WIN * b + at:WIN * b + at + n], m["view"], m["key"], [("win%d.%d" % (t, b), at, at + n)], n)
 
-    def exchange(t):
+    def send(t, second):
         dest = T.cores[rank ^ (1 << t)]
         rel = relays_of(core, dest, topo)
-        en = hop_engines(core, rel, topo)
-        ids = [topo.addr(k, core) for k in rel]
-        hq, hs, rc, rs = T["hq%d" % t], T["hs%d" % t], T["rc%d" % t], T["rs%d" % t]
-        h = G // 2
+        transfers = plan(t, second)
+        en = hop_engines(core, rel, transfers, topo)
+        ids = [topo.addr(rel[k], core) for k, lo, n in transfers]
+        land = T[("rb%d" if second else "ra%d") % t]
+        sides = [(T["hs%d" % t][:, :], T["rs%d" % t][:, :]) if lo is None else
+                 (T["hq%d" % t][:, lo:lo + n].bitcast(dt.uint8), land[:, 0:n].bitcast(dt.uint8)) for k, lo, n in transfers]
+        sem = T.sem[("arrb%d" if second else "arra%d") % t]
+        i = op("g", lambda e, q: e.remote_dma_fused(
+            [RemoteDMATransfer(dst_ids=[DstId(rid=ids[k][0], pnc=ids[k][1])], dma_engine_mask=mask_of(en[k]), remote_sem=sem,
+                               src=sides[k][0], dst=sides[k][1]) for k in range(len(transfers))], local_sem=T.sem["sent"]),
+            [("hq%d" % t, 0, 2 * A if second else A)], (), ("send", t, second))
+        sent[0] += sum(len(x) for x in en)
+        return i
 
-        def f(e, q):
-            e.remote_dma_fused([RemoteDMATransfer(dst_ids=[DstId(rid=ids[k][0], pnc=ids[k][1])], dma_engine_mask=mask_of(en[k]), remote_sem=T.sem["rarr%d" % t],
-                                                  src=hq[:, h * k:h * k + h].bitcast(dt.uint8), dst=rc[:, :].bitcast(dt.uint8)) for k in range(2)], local_sem=T.sem["sent"])
-            return e.remote_dma(rs[:, :], hs[:, 0:G], T.sem["rarr%d" % t], T.sem["sent"], ids[2][1], ids[2][0], mask_of(en[2]))
-        i = op("g", f, [("hq%d" % t, 0, G)], (), 0.6)
-        op(None, None, (), full("gq%d" % t), 0.0, sem="garr%d" % t, val=sum(len(topo.engines(k, core)) for k in relays_of(dest, core, topo)),
-           lat=HOPS + (FIRST if t == 0 else 0.0), after=[i])
-        return sum(len(x) for x in en)
+    def arrival(t, calls):
+        rel = relays_of(T.cores[rank ^ (1 << t)], core, topo)
+        op(None, None, (), full("gq%d" % t), ("arrive", t), sem="garr%d" % t, after=calls,
+           val=sum(len(topo.engines(rel[k], core)) for k, lo, n in plan(t, False) + plan(t, True)))
 
-    def scan(dst, src, a, r, cc="cc", n=C):
-        op("v", lambda e, q: e.tensor_tensor_scan(T[dst][:], T[cc][:], T[src][:, a:a + C], 0.0, ADD, MAX), r + full(cc), full(dst), el(n))
+    def scan(dst, src, a, lo, cc, kind):
+        op("v", lambda e, q: e.tensor_tensor_scan(T[dst][:, lo:lo + H], T[cc][:], T[src][:, a + lo:a + lo + H], 0.0, ADD, MAX),
+           [(src, a + lo, a + lo + H)] + full(cc), [(dst, lo, lo + H)], (kind, H))
+
+    def offsets(dst, t, sc, src, a, lo, k, kind):
+        scan(sc, src, a, lo, "c16", kind)
+        u, v = 24 * t + lo // 16, 24 * t + (lo + H) // 16
+        ts(T[dst][:, u:v], T[sc][:, lo + 15:lo + H:16], T[k][:, 0:1], None, SUB, None, [(sc, lo, lo + H)] + full(k), [(dst, u, v)])
 
     def nxrow(t):
-        return (0, C) if t == 0 else (WIN + C * (t - 1), WIN + C * t)
+        return 0 if t == 0 else WIN + C * (t - 1)
+
+    def scores(t, lo):
+        m = mm("uq16", "us16", 0, "zq%d" % t, "zs%d" % t, lo, lo + H)
+        copy(lambda: T.S[:, lo:lo + H], m["view"], m["key"], [("S", lo, lo + H)], H)
 
     def swap_links(t):
-        a, nt = slice(24 * t, 24 * t + 24), slice(24 * t + 24, 24 * t + 48)
-        tiny = el(24)
+        a = slice(24 * t, 24 * t + 24)
 
         def me(*names):
             return [(n, t, t + 1) for n in names]
 
-        def nxt(*names):
-            return [(n, t + 1, t + 2) for n in names]
-        df = ("df", WIN * t, WIN * t + WIN)
-        gather(T.dnr[:], T.df[:, df[1]:df[2]], T.pvo[:, a], me("pvo") + [df], full("dnr"), C)
-        scan("scd", "dnr", 0, full("dnr"))
-        minus(T.dn[:, a], T.scd[:, 15:C:16], "kq", "nkq", full("scd"), me("dn"))
-        times(T.dk[:, a], T.dn[:, a], "kk", me("dn"), me("dk"))
-        tt(T.db[:, a], T.pf[:, a], T.dk[:, a], SUB, me("pf", "dk"), me("db"), tiny)
-        for lo, n in ((0, H), (H, C - H)):
-            m = mm("uq16", "us16", 0, "zq%d" % t, "zs%d" % t, lo, lo + n)
-            op("v", lambda e, q, m=m, lo=lo, n=n: e.tensor_tensor(T.T1[:, lo:lo + n], m["view"](), T.D[:, C * t + lo:C * t + lo + n], MUL),
-               m["key"] + me("D"), [("T1", lo, lo + n)], el(n))
-            copy(lambda lo=lo, n=n: T.NT1[:, lo:lo + n], lambda lo=lo, n=n: T.T1[:, lo:lo + n], [("T1", lo, lo + n)], [("NT1", lo, lo + n)], n, scale=-1.0)
-        tt(T.sw[:, 0:C], T.T1[:].indirect(T.pro[:, a]), T.NT1[:], LT, full("T1", "NT1", "pro"), [("sw", 0, C)], 0.05 + C * GATHER * CY)
-        gather(T.swp[:], T.sw[:], T.pvo[:, a], me("pvo") + [("sw", 0, WIN)], full("swp"), C)
-        scan("scq", "swp", 0, full("swp"), "ccb", C // 2)
-        tt(T.pa[:, a], T.scq[:, 15:C:16], T.dn[:, a], MUL, full("scq") + me("dn"), me("pa"), tiny)
-        tt(T.pf[:, nt], T.pa[:, a], T.db[:, a], ADD, me("pa", "db"), nxt("pf"), tiny)
-        copy(lambda: T.pvo[:, nt], lambda: T.pf[:, nt], nxt("pf"), nxt("pvo"), 24, "v")
-        scan("scs", "sw", 0, [("sw", 0, C)], "ccb", C // 2)
-        tt(T.ta[:, a], T.scs[:, 15:C:16], T.dpr[:, a], MUL, full("scs", "dpr"), me("ta"), tiny)
-        tt(T.tb[:, a], T.ta[:, a], T.base[:, a], ADD, me("ta") + full("base"), me("tb"), tiny)
+        def part(name, lo):
+            return T[name][:, 24 * t + lo // 16:24 * t + (lo + H) // 16]
+        for lo in (0, H):
+            gather(T.SL[:, lo:lo + H], T.S[:], part("loo", lo), full("S", "loo"), [("SL", lo, lo + H)], H)
+            tt(T.sw[:, lo:lo + H], T.S[:].indirect(part("hio", lo)), T.SL[:, lo:lo + H], GT, full("S", "hio") + [("SL", lo, lo + H)], [("sw", lo, lo + H)], ("g", H))
+            scan("scs", "sw", 0, lo, "c16", "h")
+        tt(T.ta[:, a], T.scs[:, 15:C:16], T.dpr[:, a], MUL, full("scs", "dpr"), me("ta"), ("tt", 24))
+        tt(T.tb[:, a], T.ta[:, a], T.base[:, a], ADD, me("ta") + full("base"), me("tb"), ("tt", 24))
         copy(lambda: T.so[:, a], lambda: T.tb[:, a], me("tb"), me("so"), 24, "v")
-        (u, v), (c, d) = nxrow(t), nxrow(t + 1)
-        gather(T.nxr[:, c:d], T.nxr[:, u:v], T.so[:, a], me("so") + [("nxr", u, v)], [("nxr", c, d)], C)
-        scan("scn", "nxr", c, [("nxr", c, d)])
-        ts(T.nxl[:, nt], T.scn[:, 15:C:16], T.kq[:, 0:1], None, SUB, None, full("scn", "kq"), nxt("nxl"))
+        u, c = nxrow(t), nxrow(t + 1)
+        for lo in (0, H):
+            gather(T.sr[:, lo:lo + H], T.J[:, 0:C], part("so", lo), me("so") + full("J"), [("sr", lo, lo + H)], H, bias=-float(MID))
+        for lo in (0, H):
+            gather(T.nxr[:, c + lo:c + lo + H], T.nxr[:, u:u + C], part("so", lo), me("so") + [("nxr", u, u + C)], [("nxr", c + lo, c + lo + H)], H)
+            offsets("nxl", t + 1, "scn", "nxr", c, lo, "k16", "e")
+            gather(T.pvh[:, lo:lo + H], T.sr[:], part("pvo", lo), [("pvo", 24 * t + lo // 16, 24 * t + (lo + H) // 16)] + full("sr"), [("pvh", lo, lo + H)], H)
+            offsets("pvo", t + 1, "sch", "pvh", 0, lo, "k16p", "h")
 
-    for out, src, key, lat in (
-            (T.nxi[:], T.nx[:], full("nxi"), 2.1), (T.xw[:, 0:4 * C], T.x[:], [("xw", 0, 4 * C)], 3.8), (T.xw[:, 4 * C:4 * WIN], T.gh[:], [("xw", 4 * C, 4 * WIN)], 4.8),
-            (T.pri[:], T.pr[:], full("pri"), 5.2), (T.wq[:].bitcast(dt.uint8), T.wc[:], full("wq"), 6.5), (T.wsc[:], T.ws[:], full("wsc.load"), 7.0),
-            (T.ut[:], T.u[:], full("ut"), 7.8), (T.vt[:], T.v[:], full("vt"), 8.6)):
-        move(out, src, (), key, lat)
+    def planes(lo, hi):
+        return [("win0.%d" % b, lo, hi) for b in range(4)]
+    for out, src, key, size in (
+            (T.nxi[:], T.nx[:], full("nxi"), 144), (T.win0[:, 0:4 * C], T.x[:], planes(0, C), 8 * C), (T.win0[:, 4 * C:4 * WIN], T.gh[:], planes(C, WIN), 8 * G),
+            (T.wq[:].bitcast(dt.uint8), T.wc[:], full("wq"), 2048), (T.wsc[:], T.ws[:], full("wsc.load"), 512), (T.pri[:], T.pr[:], full("pri"), 288),
+            (T.ut[:], T.u[:], full("ut"), 1024)):
+        move(out, src, (), key, size)
 
     iota(T.pi[:], [[0, 1]], 0, 1, full("pi"), 1, small=False)
-    iota(T.jm[:], [[0, C // 16], [2 * KILL, 16]], 0, 0, full("jm"), C)
     iota(T.t4[:], [[1, 4]], 0, 0, full("t4"), 4)
-    op("v", lambda e, q: e.memset(T.half[:], 0.5), (), full("half"), el(WIN))
-    op("v", lambda e, q: e.tensor_tensor_scan(T.J[:], T.half[:], T.half[:], -1.0, ADD, ADD), full("half"), full("J"), el(WIN))
+    iota(T.jm16[:], [[0, H // 16], [1, 16]], 0, 0, full("jm16"), H)
+    iota(T.J[:, 0:MID], [[1, MID]], 0, 0, [("J", 0, MID)], MID)
+    op("s", lambda e, q: e.activation(T.J[:, MID:WIN], T.J[:, 0:MID], ACT.Copy, bias=float(MID)), [("J", 0, MID)], [("J", MID, WIN)], ("e", MID))
     iota(T.jo[:], [[0, R], [16, 24]], 0, 0, full("jo"), 72)
     iota(T.uo[:], [[16, 8]], 0, 0, full("uo"), 8, small=False)
-    iota(T.J2[:], [[1, C]], 0, 0, full("J2"), C)
-    iota(T.sw[:, C:WIN], [[0, G]], 0, 0, [("sw", C, WIN)], G)
-    for k in range(R):
-        iota(T.df[:, WIN * k + C:WIN * k + WIN], [[0, G]], 0, 0, [("df", WIN * k + C, WIN * k + WIN)], G)
-    ts(T.qi[:], T.pi[:], 15, None, AND, None, full("pi"), full("qi"))
-    copy(lambda: T.qf[:], lambda: T.qi[:], full("qi"), full("qf"), 1, "v")
-    ts(T.kq[:], T.qf[:], -float(STEP), 15.0 * STEP, MUL, ADD, full("qf"), full("kq"))
-    ts(T.kk[:], T.qf[:], -2.0, 30.0, MUL, ADD, full("qf"), full("kk"))
-    ts(T.kq4[:], T.t4[:], -0.25, T.kq[:, 0:1], MUL, ADD, full("t4", "kq"), full("kq4"))
-    ts(T.nkq[:], T.kq[:], -1.0, None, MUL, None, full("kq"), full("nkq"))
-    ts(T.qk[:], T.qf[:], 2.0 * KILL, float(KILL), MUL, ADD, full("qf"), full("qk"))
-    ts(T.cc[:], T.jm[:], T.qk[:, 0:1], float(STEP), SUB, MIN, full("jm", "qk"), full("cc"), C)
-    copy(lambda: T.ccb[:], lambda: T.cc[:], full("cc"), full("ccb"), C, "s", 2.0 / STEP)
-    ts(T.e4[:], T.pi[:], -4.0, -4.0, MUL, ADD, full("pi"), full("e4"))
-    op("s", lambda e, q: e.activation(T.ab[:], T.J[:, 0:528], ACT.Abs, bias=T.e4[:, 0:1]), full("J", "e4"), full("ab"), el(528))
-    op("s", lambda e, q: e.activation(T.ee[:], T.ab[:], ACT.Relu, bias=1.0, scale=-1.0), full("ab"), full("ee"), el(528))
+    iota(T.sr[:, C:WIN], [[1, G]], C - MID, 0, [("sr", C, WIN)], G)
+    for t in range(R):
+        iota(T["h%d" % t][:, 4 * G:8 * A], [[0, 8 * A - 4 * G]], 0, 0, [("h%d.%d" % (t, b), G, 2 * A) for b in range(4)], 8 * A - 4 * G)
+    iota(T.e4[:], [[0, 1]], -4, -4, full("e4"), 1)
+    op("s", lambda e, q: e.activation(T.ab[:], T.J[:, 0:528], ACT.Abs, bias=T.e4[:, 0:1]), full("J", "e4"), full("ab"), ("e", 528))
+    op("s", lambda e, q: e.activation(T.ee[:], T.ab[:], ACT.Relu, bias=1.0, scale=-1.0), full("ab"), full("ee"), ("e", 528))
     for b in range(4):
         quant("eq", "es", 128 * b, 128 * b + 128, "ee", 4 - b, 516 - b, full("ee"))
+    ts(T.qi[:], T.pi[:], 15, None, AND, None, full("pi"), full("qi"))
+    copy(lambda: T.qf[:], lambda: T.qi[:], full("qi"), full("qf"), 1, "v")
+    affine("q1", "qf", 1.0, 1.0)
+    ts(T.k16[:], T.qf[:], 15.0, float(S16), LT, MUL, full("qf"), full("k16"))
+    affine("k16p", "k16", 1.0, -float(MID))
+    ts(T.kq4[:], T.t4[:], -0.25, T.k16[:, 0:1], MUL, ADD, full("t4", "k16"), full("kq4"))
+    ts(T.ca[:, 0:H], T.jm16[:], T.q1[:, 0:1], float(S16), EQ, MUL, full("jm16", "q1"), [("ca", 0, H)], H, "h")
+    ts(T.ca[:, H:C], T.jm16[:], T.qf[:, 0:1], -float(K16), EQ, MUL, full("jm16", "qf"), [("ca", H, C)], H, "h")
+    tt(T.c16[:], T.ca[:, 0:H], T.ca[:, H:C], ADD, full("ca"), full("c16"), ("tt", H))
 
     copy(lambda: T.nxo[:], lambda: T.nxi[:], full("nxi"), full("nxo"), 36, "v")
+    op("v", lambda e, q: e.tensor_copy(T.pvr[:].indirect(T.nxo[:]), T.J[:]), full("J", "nxo"), full("pvr"), ("scatter", WIN))
+    for lo in (0, H, C):
+        gather(T.nxr[:, lo:lo + H], T.J[:], T.nxo[:, lo // 16:(lo + H) // 16], full("J", "nxo"), [("nxr", lo, lo + H)], H)
     for b in range(4):
-        ts(T.nx4[:, 24 * b:24 * b + 24], T.nxi[:, 0:24], 4.0, float(b), MUL, ADD, full("nxi"), [("nx4", b, b + 1)])
-    op("v", lambda e, q: e.tensor_copy(T.pvr[:].indirect(T.nxo[:]), T.J[:]), full("J", "nxo"), full("pvr"), 0.05 + WIN * SCATTER * CY)
-    gather(T.nxr[:, 0:WIN], T.J[:], T.nxo[:], full("J", "nxo"), [("nxr", 0, WIN)], WIN, "s")
-    scan("scp", "pvr", 0, full("pvr"))
+        ts(T.nx4[:, 24 * b:24 * b + 24], T.nxi[:, 0:24], 4.0, float(b), MUL, ADD, full("nxi"), [("nx4", 24 * b, 24 * b + 24)])
+    for lo in (0, H):
+        scan("scp", "pvr", 0, lo, "c16", "e")
     for b in range(4):
-        ts(T.pv4[:, 24 * b:24 * b + 24], T.scp[:, 15:C:16], T.kq4[:, b:b + 1], 4.0, SUB, MUL, full("scp", "kq4"), [("pv4", b, b + 1)])
-    ts(T.pvo[:, 0:24], T.scp[:, 15:C:16], T.kq[:, 0:1], None, SUB, None, full("scp", "kq"), [("pvo", 0, 1)])
-    minus(T.pf[:, 0:24], T.scp[:, 15:C:16], "kq", "nkq", full("scp"), [("pf", 0, 1)])
-    copy(lambda: T.pro[:], lambda: T.pri[:], full("pri"), full("pro"), 72, "v")
-    copy(lambda: T.prf[:], lambda: T.pri[:], full("pri"), full("prf"), 72, "v")
+        ts(T.pv4[:, 24 * b:24 * b + 24], T.scp[:, 15:C:16], T.kq4[:, b:b + 1], 4.0, SUB, MUL, full("scp", "kq4"), [("pv4", 24 * b, 24 * b + 24)])
+    ts(T.pvo[:, 0:24], T.scp[:, 15:C:16], T.k16[:, 0:1], None, SUB, None, full("scp", "k16"), [("pvo", 0, 24)])
     ts(T.joq[:], T.jo[:], T.qf[:, 0:1], None, ADD, None, full("jo", "qf"), full("joq"), 72)
-    tt(T.dpr[:], T.prf[:], T.joq[:], SUB, full("prf", "joq"), full("dpr"), el(144))
-    times(T.kd[:], T.dpr[:], "kk", full("dpr"), full("kd"), 72)
-    tt(T.base[:], T.joq[:], T.kd[:], SUB, full("joq", "kd"), full("base"), el(144))
-    for i in range(R):
-        d, key = T.df[:, WIN * i:WIN * i + C], [("df", WIN * i, WIN * i + C)]
-        tt(d, T.J[:, 0:C].indirect(T.pro[:, 24 * i:24 * i + 24]), T.J2[:], SUB, full("J", "J2", "pro"), key, 0.05 + C * GATHER * CY)
-        op("s", lambda e, q, i=i, d=d: e.activation(T.D[:, C * i:C * i + C], d, ACT.Sign), key, [("D", i, i + 1)], el(C))
+    tt(T.lof[:], T.pri[:], T.joq[:], MIN, full("pri", "joq"), full("lof"), ("tt", 72))
+    copy(lambda: T.loo[:], lambda: T.lof[:], full("lof"), full("loo"), 72, "v")
+    tt(T.hif[:], T.pri[:], T.joq[:], MAX, full("pri", "joq"), full("hif"), ("tt", 72))
+    copy(lambda: T.hio[:], lambda: T.hif[:], full("hif"), full("hio"), 72, "v")
+    tt(T.dpr[:], T.pri[:], T.joq[:], SUB, full("pri", "joq"), full("dpr"), ("tt", 72))
+    times(T.kd[:], T.dpr[:], "k16", full("dpr"), full("kd"), 72)
+    tt(T.base[:], T.joq[:], T.kd[:], SUB, full("joq", "kd"), full("base"), ("tt", 72))
     quant("uq", "us", 0, 128, "ut", 0, 512, full("ut"))
     copy(lambda: T.uof[:], lambda: T.uo[:], full("uo"), full("uof"), 8, "v")
     op("v", lambda e, q: e.tensor_copy(T.uq16[:, 0:128].bitcast(dt.uint32), T.uq[:, 0:128].bitcast(dt.uint32).indirect(T.uof[:, 0:8])),
-       full("uq", "uof"), full("uq16"), 0.05 + 128 * GATHER * CY)
+       full("uq", "uof"), full("uq16"), ("g", 128))
     gather(T.us16[:, 0:128], T.us[:, 0:128], T.uof[:, 0:8], full("uq", "uof"), full("us16.load"), 128)
-    quant("vq", "vs", 0, 128, "vt", 0, 512, full("vt"))
 
-    sent = 0
+    sent = [0]
     for t in range(R):
-        read(t, 0, H)
-        layer(t, 0, H)
-        sent += exchange(t)
-        read(t, H, C - H)
+        read(t, 0, FIRST_PIECES)
+        quant_z(t, 0, A)
+        layer(t, 0, A, 0, A, "h", 0, A)
+        s1 = send(t, False)
+        quant_z(t, G - A, A)
+        layer(t, G - A, G, A, B, "h", A, A)
+        arrival(t, [s1, send(t, True)])
+        scores(t, 0)
+        read(t, H, REST_PIECES)
+        quant_z(t, H, C - H)
+        scores(t, H)
         swap_links(t)
-        layer(t, H, C - H)
-        unpack(t + 1, 0, "hq%d" % t, "hs%d" % t, 0, H)
-        unpack(t + 1, H, "hq%d" % t, "hs%d" % t, H, C - H)
-        unpack(t + 1, C, "gq%d" % t, "gs%d" % t, 0, G)
-    c, d = nxrow(R)
-    move(T.nl[:, C:WIN], T.nxr[0:128:16, C:WIN], [("nxr", C, WIN)], [("nl", C, WIN)])
-    move(T.nl[:, 0:C], T.nxr[0:128:16, c:d], [("nxr", c, d)], [("nl", 0, C)])
+        layer(t, H, C, H, C - H, "k", 0, C - H)
+        unpack(t + 1, 0, "hq%d" % t, "hs%d" % t, H)
+        unpack(t + 1, H, "kq%d" % t, "ks%d" % t, C - H)
+        unpack(t + 1, C, "gq%d" % t, "gs%d" % t, G)
+    move(T.vt[:], T.v[:], [("so", 0, 1)], full("vt"), 1024)
+    quant("vq", "vs", 0, 128, "vt", 0, 512, full("vt"))
+    c = nxrow(R)
+    move(T.nl[:, C:WIN], T.nxr[0:128:16, C:WIN], [("nxr", C, WIN)], [("nl", C, WIN)], 64)
+    move(T.nl[:, 0:C], T.nxr[0:128:16, c:c + C], [("nxr", c, c + C)], [("nl", 0, C)], 128)
     zq, zs, qn = T["zq%d" % R], T["zs%d" % R], "zq%d" % R
-    for lo, n in ((0, 256), (256, 128)):
-        read(R, lo, n)
+    read(R, 0, LAST_PIECES)
+    lo = 0
+    for n in LAST_TILES:
+        quant_z(R, lo, n)
         m = mm("vq", "vs", 0, qn, "zs%d" % R, lo, lo + n)
-        move(T.oc[:, 4 * lo:4 * (lo + n)], zq[:, lo:lo + n].bitcast(dt.uint8), [(qn, lo, lo + n)], [("oc", lo, lo + n)], 2.3)
+        move(T.oc[:, 4 * lo:4 * (lo + n)], zq[:, lo:lo + n].bitcast(dt.uint8), [(qn, lo, lo + n)], [("oc", lo, lo + n)], 4 * n)
         copy(lambda lo=lo, n=n: T.y_sb[:, lo:lo + n], m["view"], m["key"], [("y_sb", lo, lo + n)], n)
-        move(T.y[:, lo:lo + n], T.y_sb[:, lo:lo + n], [("y_sb", lo, lo + n)], [("y", lo, lo + n)], 2.3)
+        move(T.y[:, lo:lo + n], T.y_sb[:, lo:lo + n], [("y_sb", lo, lo + n)], [("y", lo, lo + n)], 4 * n)
+        lo += n
     for k in range(4):
-        move(T.osc[4 * k:4 * k + 4, :], zs[32 * k:32 * k + 4, :], [(qn, 0, C)], [("osc", k, k + 1)], q="s")
-    op("y", None, [("oc", 0, C), ("y", 0, C), ("osc", 0, 4), ("nl", 0, WIN)], (), 0.0)
+        move(T.osc[4 * k:4 * k + 4, :], zs[32 * k:32 * k + 4, :], [(qn, 0, C)], [("osc", k, k + 1)], 64, q="s")
+    op("y", None, [("oc", 0, C), ("y", 0, C), ("osc", 0, 4), ("nl", 0, WIN)], (), ("end", 0))
+    return ops, sent[0]
+
+
+def rank_program(g, core, T, topo):
+    rank = T.rank_of(core)
+    if rank is None:
+        return relay_program(g, core, T, topo)
+    ops, sent = calls_of(core, rank, T, topo)
     emit(g, T, arrange(ops))
     g.wait_ge(T.sem.sent, sent)

@@ -3,43 +3,52 @@ from concourse.mybir import dt, AluOpType, ActivationFunctionType
 
 C, G, R, WIN = 384, 192, 3, 576
 H, A, B = G, 128, 64
-MID = WIN // 2
-S16, K16 = 640, 2048
+UNIT = 1024.0
+BIG = 4096.0 * 3072.0
 F8, BF, F16, F32, I32, U16, U8 = "float8_e4m3fn_x4", "bfloat16", "float16", "float32", "int32", "uint16", "uint8"
-FIRST_PIECES, REST_PIECES, LAST_PIECES, LAST_TILES = (128, 64), (192,), (256, 128), (256, 128)
-ON_VECTOR = (29, 123, 125, 128, 167, 170, 182, 221, 225, 232, 233, 267, 273, 275, 277, 290, 329, 330, 340, 347, 350, 381, 390, 414)
-ORDER = [int(k) for k in """
-0 5 1 2 13 7 59 25 26 28 3 4 6 27 9 10 29 11 31 32 18 8 14 15 16 12 17 33 34 40 41 42 35 30 43 44 39 19 38 36 37 66 64 62 68 70 72
-76 74 47 45 46 48 67 65 63 69 71 109 103 78 81 85 83 79 82 86 84 80 107 77 75 73 58 110 60 89 87 105 90 94 96 92 95 61 97 91 93 101
-20 102 104 108 106 50 111 112 98 51 53 52 23 21 54 24 55 113 114 117 115 118 141 143 137 146 139 152 150 144 138 56 142 140 147 153
-151 116 119 57 120 49 121 22 88 99 100 122 145 148 156 154 158 160 124 388 386 123 131 134 159 161 155 157 149 166 162 168 164 125
-128 132 126 133 129 127 135 167 163 174 169 165 176 172 178 130 136 182 211 170 183 175 171 177 180 184 217 173 179 186 212 181 185
-218 187 193 191 189 188 215 213 190 194 192 197 216 214 198 204 200 202 199 201 205 203 209 195 210 219 220 196 206 387 207 208 221
-225 251 252 222 226 223 227 224 247 258 259 248 249 260 250 261 245 254 246 255 256 257 228 229 230 253 231 239 232 233 266 268 264
-262 236 242 269 263 265 267 234 240 274 237 235 241 238 243 275 244 276 270 272 282 271 290 277 284 291 283 273 278 280 286 323 288
-292 319 285 279 281 287 294 324 289 293 320 299 297 301 295 321 325 298 300 296 302 305 310 312 308 306 309 311 313 307 322 326 317
-303 327 328 304 314 353 315 318 355 359 357 368 366 364 329 362 330 316 354 333 331 334 332 335 336 337 338 356 360 369 358 367 361
-365 363 376 374 372 370 340 339 341 347 377 344 371 373 378 384 380 382 379 350 348 342 351 345 349 343 352 346 375 385 396 390 381
-383 392 391 397 393 394 395 398 404 400 402 406 407 399 405 403 401 409 411 412 389 408 410 413 414 416 419 418 417 415 420""".split()]
+PIECES, SCORES, UNPACKS, LAST_TILES = (128, 128, 128), (256, 128), (256, 128), (128, 128, 128)
+PAIR_PIECES, LINK_PIECES, ROW_PIECES, TS = (192, 192), (192, 192), (192, 192), (192, 192)
+PP = {}
+PLAN = """
+0 8 7 18 19 24 27 25 28 13 15 9 -10 26 11 29 2 1 23 21 20 14 16 68 22 4 6 3 5 12 30 17 38 39 32 31 59 34 -33 35 40 45 46 47 41 36
+48 80 72 37 49 51 71 50 52 53 73 81 75 74 84 83 77 86 87 78 82 54 67 89 96 90 94 92 97 91 76 85 88 100 95 93 107 101 70 42 105
+103 98 108 69 79 99 102 106 122 60 111 104 55 109 124 118 64 61 123 110 125 65 119 112 62 56 -113 63 66 116 114 151 155 126 128
+149 153 127 129 130 117 152 156 44 43 131 57 132 -115 133 58 134 120 -135 159 163 157 161 389 -139 154 150 136 137 160 164 140
+-138 142 145 141 146 144 121 143 165 167 147 148 169 162 158 166 171 168 -173 170 -179 172 185 174 180 191 186 175 181 193 192
+176 187 183 182 197 194 188 184 198 200 204 202 177 189 195 199 201 205 203 208 178 190 196 211 215 209 213 206 230 212 216 210
+219 214 207 232 231 390 217 224 233 218 -236 225 237 222 226 220 223 234 227 263 221 264 235 257 261 259 258 262 260 239 238 228
+240 241 267 268 242 271 265 272 266 269 -244 -247 243 245 -270 246 250 249 248 252 253 254 251 255 256 229 275 273 276 277 274
+279 278 281 -287 -289 280 288 293 299 283 290 282 294 300 301 295 285 284 305 302 296 286 306 308 312 310 316 291 297 303 307 309
+313 311 292 298 304 317 319 321 323 318 320 314 322 327 338 324 315 325 339 326 340 341 334 328 -344 332 367 330 365 -333 371 369
+335 342 329 368 331 345 343 347 346 336 348 349 350 373 377 379 366 372 370 374 -351 -353 375 378 380 376 352 355 -356 354 391
+357 358 362 359 361 360 364 363 337 383 384 381 382 -399 -397 392 385 387 386 393 388 400 405 398 394 411 406 412 403 404 409 415
+407 417 418 410 395 401 420 413 416 419 408 427 396 402 414 428 421 429 430 422 423 431 424 432 435 434 -425 426 433 436
+""".split()
+ORDER = [abs(int(k)) for k in PLAN]
+ON_VECTOR = [-int(k) for k in PLAN if k[0] == "-"]
 
 SCRATCH = {n: ("sbuf", [128, w], d) for n, w, d in (
     ("nxi", 36, I32), ("pri", 72, I32), ("win0", 4 * WIN, BF), ("ut", 512, BF), ("vt", 512, BF), ("wq", 512, F8), ("wsc", 512, U8),
-    ("J", WIN, F32), ("e4", 1, F32), ("pi", 1, I32), ("qi", 1, I32), ("qf", 1, F32), ("q1", 1, F32), ("t4", 4, F32), ("kq4", 4, F32),
-    ("k16", 1, F32), ("k16p", 1, F32), ("jm16", H, BF), ("ca", C, F16), ("c16", H, F16),
+    ("J0", WIN // 4, F32), ("J", WIN, F32), ("pf", 2, F32), ("qa", 1, F32), ("qb", 1, F32), ("q2", 1, F32),
+    ("oa", 1, F32), ("ob", 1, F32), ("odd", 1, F32), ("jm", H, BF), ("sg", H, BF),
+    ("cm", 2 * H, F16), ("ca", H, F16), ("hh", 24, F32), ("zz", 32, F32), ("mu", 24, F32),
+    ("m4", 1, F32), ("b4", 1, F32), ("k16", 1, F32),
     ("jo", 72, F32), ("joq", 72, F32), ("uo", 8, I32), ("uof", 8, U16),
-    ("ab", 528, BF), ("ee", 528, BF), ("eq", 512, F8), ("es", 512, U8),
+    ("ee", 516, BF), ("eq", 512, F8), ("es", 512, U8),
     ("uq", 128, F8), ("us", 128, U8), ("uq16", 128, F8), ("us16", 128, U8), ("vq", 128, F8), ("vs", 128, U8),
-    ("nxo", 36, U16), ("nx4", 96, U16), ("pv4", 96, U16), ("pvo", 96, U16), ("nxl", 96, U16), ("so", 72, U16), ("loo", 72, U16), ("hio", 72, U16),
+    ("nxo", 36, U16), ("nx4", 96, U16), ("pva", 48, U16), ("pvb", 48, U16), ("pvo", 96, U16), ("nxl", 96, U16),
+    ("so", 72, U16), ("loo", 72, U16), ("hio", 72, U16),
     ("dpr", 72, F32), ("kd", 72, F32), ("base", 72, F32), ("lof", 72, F32), ("hif", 72, F32), ("ta", 72, F32), ("tb", 72, F32),
-    ("nxr", WIN + 3 * C, F32), ("pvr", WIN, F32), ("sr", WIN, F32), ("pvh", C, F16), ("S", C, F32), ("SL", C, F32), ("sw", C, F16),
-    ("scn", C, F32), ("scp", C, F32), ("sch", C, F16), ("scs", C, F16), ("y_sb", C, F32))}
+    ("nxr", 3 * C, F32), ("nxh", C, F16), ("nlr", WIN, F32), ("pvr", WIN, F32), ("sr", WIN, F32), ("pvh", C, F16), ("pvf", C, F16),
+    ("S", C, F32), ("SL", C, F32), ("sw", C, F16),
+    ("scn", C, F16), ("scp", C, F16), ("sch", C, F16), ("scs", C, F16), ("y_sb", C, F32),
+    ("P0", 4 * C, BF), ("P1", 4 * C, BF), ("h", 4 * C, BF))}
 for _t in range(R + 1):
-    SCRATCH.update({"%s%d" % (n, _t): ("sbuf", [128, w], d) for n, w, d in (("P", 4 * C, BF), ("z", 4 * C, BF), ("zq", C, F8), ("zs", C, U8))})
+    SCRATCH.update({"%s%d" % (n, _t): ("sbuf", [128, w], d) for n, w, d in (("z", 4 * C, BF), ("zq", C, F8), ("zs", C, U8))})
     if _t < R:
         SCRATCH["win%d" % (_t + 1)] = ("sbuf", [128, 4 * WIN], BF)
         SCRATCH.update({"%s%d" % (n, _t): ("sbuf", [128, w], d) for n, w, d in (
-            ("h", 8 * A, BF), ("hq", 2 * A, F8), ("hs", 2 * A, U8), ("k", 4 * H, BF), ("kq", H, F8), ("ks", H, U8),
-            ("ra", B, F8), ("rb", B, F8), ("rs", 4 * B, U8), ("gq", G, F8), ("gs", G, U8))})
+            ("hq", C, F8), ("hs", C, U8), ("ra", B, F8), ("rb", B, F8), ("rs", 4 * B, U8), ("gq", G, F8), ("gs", G, U8))})
 for _b in range(8):
     SCRATCH["pb%d" % _b] = ("psum", [128, 512], F32)
 
@@ -190,7 +199,7 @@ def emit(g, T, ops):
 def calls_of(core, rank, T, topo):
     ops = []
     ADD, SUB, MUL, MAX, MIN = AluOpType.add, AluOpType.subtract, AluOpType.mult, AluOpType.max, AluOpType.min
-    LT, GT, EQ, AND = AluOpType.is_lt, AluOpType.is_gt, AluOpType.is_equal, AluOpType.bitwise_and
+    GT = AluOpType.is_gt
     ACT = ActivationFunctionType
 
     def op(q, f, r, w, c, **kw):
@@ -200,18 +209,21 @@ def calls_of(core, rank, T, topo):
     def full(*names):
         return [(n, 0, 1 << 20) for n in names]
 
-    def move(out, src, r, w, size, q="y"):
-        op(q, lambda e, q: e.dma_start(out, src), r, w, ("dma", size))
+    def runs(pieces, lo=0):
+        out = []
+        for n in pieces:
+            out.append((lo, n))
+            lo += n
+        return out
+
+    def move(out, src, r, w, size, q="y", rows=128):
+        op(q, lambda e, q: e.dma_start(out, src), r, w, ("dma", size, rows))
 
     def copy(out, in_, r, w, n, q="vs"):
         op(q, lambda e, q: e.tensor_copy(out(), in_()) if q == "v" else e.activation(out(), in_(), ACT.Copy), r, w, ("e", n))
 
-    def gather(out, win, off, r, w, n, q="vs", bias=None):
-        def f(e, q):
-            if bias is None:
-                return e.tensor_copy(out, win.indirect(off)) if q == "v" else e.activation(out, win.indirect(off), ACT.Copy)
-            return e.tensor_scalar(out, win.indirect(off), bias, None, ADD) if q == "v" else e.activation(out, win.indirect(off), ACT.Copy, bias=bias)
-        op(q, f, r, w, ("g", n))
+    def gather(out, win, off, r, w, n):
+        op("vs", lambda e, q: e.tensor_copy(out, win.indirect(off)) if q == "v" else e.activation(out, win.indirect(off), ACT.Copy), r, w, ("g", n))
 
     def tt(out, a, b, o, r, w, c):
         op("v", lambda e, q: e.tensor_tensor(out, a, b, o), r, w, c)
@@ -222,13 +234,9 @@ def calls_of(core, rank, T, topo):
         else:
             op("v", lambda e, q: e.tensor_scalar(out, a, s1, s2, o1, o2), r, w, (kind, n))
 
-    def times(out, a, col, r, w, n=64):
-        op("vs", lambda e, q: e.tensor_scalar(out, a, T[col][:, 0:1], None, MUL) if q == "v" else
-           e.activation(out, a, ACT.Identity, scale=T[col][:, 0:1]), r + full(col), w, ("e", n))
-
-    def affine(out, a, s, b):
-        op("vs", lambda e, q: e.tensor_scalar(T[out][:], T[a][:], s, b, MUL, ADD) if q == "v" else
-           e.activation(T[out][:], T[a][:], ACT.Copy, scale=s, bias=b), full(a), full(out), ("e", 1))
+    def affine(out, a, s, b, r, w, n, kind="e"):
+        func = ACT.Copy if isinstance(s, float) and isinstance(b, float) else ACT.Identity
+        op("vs", lambda e, q: e.tensor_scalar(out, a, s, b, MUL, ADD) if q == "v" else e.activation(out, a, func, scale=s, bias=b), r, w, (kind, n))
 
     def iota(out, pat, base, cm, w, n, small=True):
         if small:
@@ -246,37 +254,46 @@ def calls_of(core, rank, T, topo):
         m = {"key": full("@%d" % made[0])}
         op("p", lambda e, q: e.matmul_mx(T[m["k"]][:, 0:b - a], T[wn][:, wa:wa + 128], T[wsn][:, wa:wa + 128], T[xn][:, a:b], T[xsn][:, a:b], True, True),
            [(wn, wa, wa + 128), (wsn + ".load", 0, 1), (xn, a, b)], m["key"], ("mm", b - a), m=m)
-        m["view"] = lambda lo=a, hi=b: T[m["k"]][:, lo - a:hi - a]
+        m["view"] = lambda: T[m["k"]][:, 0:b - a]
         return m
 
-    def read(t, lo, pieces):
-        for n in pieces:
-            for b in range(4):
-                if t == 0:
-                    win, l1, l2, i = T.win0[:], "nx4", "pv4", b
-                else:
-                    win, l1, l2, i = T["win%d" % t][:, WIN * b:WIN * b + WIN], "nxl", "pvo", t
-                key, u, v = ("win%d.%d" % (t, b), 0, WIN), 24 * i + lo // 16, 24 * i + (lo + n) // 16
-                P, k = T["P%d" % t][:, C * b + lo:C * b + lo + n], ("P%d" % t, C * b + lo, C * b + lo + n)
-                gather(P, win, T[l1][:, u:v], [key, (l1, u, v)], [k], n)
-                tt(T["z%d" % t][:, 4 * lo + b:4 * (lo + n):4], win.indirect(T[l2][:, u:v]), P, ADD, [key, (l2, u, v), k], [("z%d.%d" % (t, b), lo, lo + n)], ("g", n))
-            lo += n
+    def first_read():
+        for h in range(2):
+            for lo, n in runs(PP.get((0, h), PIECES)):
+                keys = [("win0.%d" % b, 0, WIN) for b in (h, h + 2)]
+                pk = [("P0.%d" % b, lo, lo + n) for b in (h, h + 2)]
+                a, l2, u = 2 * C * h + 2 * lo, ("pva", "pvb")[h], lo // 8
+                for i in range(2):
+                    c = 24 * (h + 2 * i) + lo // 16
+                    gather(T.P0[:, a + i:a + 2 * n:2], T.win0[:], T.nx4[:, c:c + n // 16], [keys[i], ("nx4", c, c + n // 16)], [pk[i]], n)
+                tt(T.z0[:, 4 * lo + h:4 * (lo + n):2], T.win0[:].indirect(T[l2][:, u:u + n // 8]), T.P0[:, a:a + 2 * n], ADD,
+                   keys + pk + [(l2, u, u + n // 8)], [("z0.%d" % b, lo, lo + n) for b in (h, h + 2)], ("g", 2 * n))
+
+    def read(t):
+        if t == 0:
+            return first_read()
+        for b in range(4):
+            for lo, n in runs(PP.get((t, b), PIECES)):
+                win, u, key, pk = T["win%d" % t][:, WIN * b:WIN * b + WIN], 24 * t + lo // 16, ("win%d.%d" % (t, b), 0, WIN), ("P%d.%d" % (t % 2, b), lo, lo + n)
+                P = T["P%d" % (t % 2)][:, C * b + lo:C * b + lo + n]
+                gather(P, win, T.nxl[:, u:u + n // 16], [key, ("nxl", u, u + n // 16)], [pk], n)
+                tt(T["z%d" % t][:, 4 * lo + b:4 * (lo + n):4], win.indirect(T.pvo[:, u:u + n // 16]), P, ADD, [key, pk, ("pvo", u, u + n // 16)],
+                   [("z%d.%d" % (t, b), lo, lo + n)], ("g", n))
 
     def quant_z(t, lo, n):
         quant("zq%d" % t, "zs%d" % t, lo, lo + n, "z%d" % t, 4 * lo, 4 * (lo + n), [("z%d.%d" % (t, b), lo, lo + n) for b in range(4)])
 
-    def layer(t, za, zb, lo, n, hn, at, wide):
-        h = "%s%d" % (hn, t)
+    def layer(t, lo, n):
         for b in range(4):
-            m, out = mm("wq", "wsc", 128 * b, "zq%d" % t, "zs%d" % t, za, zb), T[h][:, 4 * at + b:4 * (at + n):4]
-            op("vs", lambda e, q, m=m, out=out: e.activation(out, m["view"](lo, lo + n), ACT.Relu, scale=0.015625) if q == "s" else
-               e.tensor_scalar(out, m["view"](lo, lo + n), 0.0, 0.015625, MAX, MUL), m["key"], [("%s.%d" % (h, b), at, at + n)], ("e", n))
-        quant("%sq%d" % (hn, t), "%ss%d" % (hn, t), at, at + wide, h, 4 * at, 4 * (at + wide), [("%s.%d" % (h, b), at, at + wide) for b in range(4)])
+            m, out = mm("wq", "wsc", 128 * b, "zq%d" % t, "zs%d" % t, lo, lo + n), T.h[:, 4 * lo + b:4 * (lo + n):4]
+            op("vs", lambda e, q, m=m, out=out: e.activation(out, m["view"](), ACT.Relu, scale=0.015625) if q == "s" else
+               e.tensor_scalar(out, m["view"](), 0.0, 0.015625, MAX, MUL), m["key"], [("h.%d" % b, lo, lo + n)], ("e", n))
+        quant("hq%d" % t, "hs%d" % t, lo, lo + n, "h", 4 * lo, 4 * (lo + n), [("h.%d" % b, lo, lo + n) for b in range(4)])
 
-    def unpack(t, at, qn, sn, n):
+    def unpack(t, at, qn, sn, lo, n):
         for b in range(4):
-            m = mm("eq", "es", 128 * b, qn, sn, 0, n)
-            copy(lambda b=b: T["win%d" % t][:, WIN * b + at:WIN * b + at + n], m["view"], m["key"], [("win%d.%d" % (t, b), at, at + n)], n)
+            m = mm("eq", "es", 128 * b, qn, sn, lo, lo + n)
+            copy(lambda a=WIN * b + at: T["win%d" % t][:, a:a + n], m["view"], m["key"], [("win%d.%d" % (t, b), at, at + n)], n)
 
     def send(t, second):
         dest = T.cores[rank ^ (1 << t)]
@@ -285,7 +302,7 @@ def calls_of(core, rank, T, topo):
         en = hop_engines(core, rel, transfers, topo)
         ids = [topo.addr(rel[k], core) for k, lo, n in transfers]
         land = T[("rb%d" if second else "ra%d") % t]
-        sides = [(T["hs%d" % t][:, :], T["rs%d" % t][:, :]) if lo is None else
+        sides = [(T["hs%d" % t][:, 0:2 * A], T["rs%d" % t][:, :]) if lo is None else
                  (T["hq%d" % t][:, lo:lo + n].bitcast(dt.uint8), land[:, 0:n].bitcast(dt.uint8)) for k, lo, n in transfers]
         sem = T.sem[("arrb%d" if second else "arra%d") % t]
         i = op("g", lambda e, q: e.remote_dma_fused(
@@ -300,21 +317,20 @@ def calls_of(core, rank, T, topo):
         op(None, None, (), full("gq%d" % t), ("arrive", t), sem="garr%d" % t, after=calls,
            val=sum(len(topo.engines(rel[k], core)) for k, lo, n in plan(t, False) + plan(t, True)))
 
-    def scan(dst, src, a, lo, cc, kind):
-        op("v", lambda e, q: e.tensor_tensor_scan(T[dst][:, lo:lo + H], T[cc][:], T[src][:, a + lo:a + lo + H], 0.0, ADD, MAX),
-           [(src, a + lo, a + lo + H)] + full(cc), [(dst, lo, lo + H)], (kind, H))
+    def scan(dst, src, a, lo, c, o, kind):
+        op("v", lambda e, q: e.tensor_tensor_scan(T[dst][:, lo:lo + H], T[c[0]][:, c[1]:c[1] + H], T[src][:, a + lo:a + lo + H], 0.0, o, MAX),
+           [(src, a + lo, a + lo + H), (c[0], c[1], c[1] + H)], [(dst, lo, lo + H)], (kind, H))
 
-    def offsets(dst, t, sc, src, a, lo, k, kind):
-        scan(sc, src, a, lo, "c16", kind)
-        u, v = 24 * t + lo // 16, 24 * t + (lo + H) // 16
-        ts(T[dst][:, u:v], T[sc][:, lo + 15:lo + H:16], T[k][:, 0:1], None, SUB, None, [(sc, lo, lo + H)] + full(k), [(dst, u, v)])
+    def list16(dst, t, sc, src, a, kind, pieces):
+        for lo in (0, H):
+            scan(sc, src, a, lo, ("cm", 0), MUL, kind)
+        for lo, n in runs(pieces):
+            u = 24 * t + lo // 16
+            ts(T[dst][:, u:u + n // 16], T[sc][:, lo + 15:lo + n:16], T.mu[:, 15:16], -float(WIN), MUL, ADD, [(sc, lo, lo + n)] + full("mu"), [(dst, u, u + n // 16)])
 
-    def nxrow(t):
-        return 0 if t == 0 else WIN + C * (t - 1)
-
-    def scores(t, lo):
-        m = mm("uq16", "us16", 0, "zq%d" % t, "zs%d" % t, lo, lo + H)
-        copy(lambda: T.S[:, lo:lo + H], m["view"], m["key"], [("S", lo, lo + H)], H)
+    def scores(t, lo, n):
+        m = mm("uq16", "us16", 0, "zq%d" % t, "zs%d" % t, lo, lo + n)
+        copy(lambda: T.S[:, lo:lo + n], m["view"], m["key"], [("S", lo, lo + n)], n)
 
     def swap_links(t):
         a = slice(24 * t, 24 * t + 24)
@@ -322,23 +338,24 @@ def calls_of(core, rank, T, topo):
         def me(*names):
             return [(n, t, t + 1) for n in names]
 
-        def part(name, lo):
-            return T[name][:, 24 * t + lo // 16:24 * t + (lo + H) // 16]
+        def part(name, lo, n):
+            return T[name][:, 24 * t + lo // 16:24 * t + (lo + n) // 16]
+        for lo, n in runs(PAIR_PIECES):
+            gather(T.SL[:, lo:lo + n], T.S[:], part("loo", lo, n), full("S", "loo"), [("SL", lo, lo + n)], n)
+            tt(T.sw[:, lo:lo + n], T.S[:].indirect(part("hio", lo, n)), T.SL[:, lo:lo + n], GT, full("S", "hio") + [("SL", lo, lo + n)], [("sw", lo, lo + n)], ("g", n))
         for lo in (0, H):
-            gather(T.SL[:, lo:lo + H], T.S[:], part("loo", lo), full("S", "loo"), [("SL", lo, lo + H)], H)
-            tt(T.sw[:, lo:lo + H], T.S[:].indirect(part("hio", lo)), T.SL[:, lo:lo + H], GT, full("S", "hio") + [("SL", lo, lo + H)], [("sw", lo, lo + H)], ("g", H))
-            scan("scs", "sw", 0, lo, "c16", "h")
+            scan("scs", "sw", 0, lo, ("ca", 0), ADD, "h")
         tt(T.ta[:, a], T.scs[:, 15:C:16], T.dpr[:, a], MUL, full("scs", "dpr"), me("ta"), ("tt", 24))
         tt(T.tb[:, a], T.ta[:, a], T.base[:, a], ADD, me("ta") + full("base"), me("tb"), ("tt", 24))
         copy(lambda: T.so[:, a], lambda: T.tb[:, a], me("tb"), me("so"), 24, "v")
-        u, c = nxrow(t), nxrow(t + 1)
-        for lo in (0, H):
-            gather(T.sr[:, lo:lo + H], T.J[:, 0:C], part("so", lo), me("so") + full("J"), [("sr", lo, lo + H)], H, bias=-float(MID))
-        for lo in (0, H):
-            gather(T.nxr[:, c + lo:c + lo + H], T.nxr[:, u:u + C], part("so", lo), me("so") + [("nxr", u, u + C)], [("nxr", c + lo, c + lo + H)], H)
-            offsets("nxl", t + 1, "scn", "nxr", c, lo, "k16", "e")
-            gather(T.pvh[:, lo:lo + H], T.sr[:], part("pvo", lo), [("pvo", 24 * t + lo // 16, 24 * t + (lo + H) // 16)] + full("sr"), [("pvh", lo, lo + H)], H)
-            offsets("pvo", t + 1, "sch", "pvh", 0, lo, "k16p", "h")
+        for lo, n in runs(ROW_PIECES):
+            gather(T.sr[:, lo:lo + n], T.J[:, 0:C], part("so", lo, n), me("so") + full("J"), [("sr", lo, lo + n)], n)
+        row, c = ("nxr", C * t + C) if t < R - 1 else ("nxh", 0)
+        for lo, n in runs(LINK_PIECES):
+            gather(T[row][:, c + lo:c + lo + n], T.nxr[:, C * t:C * t + C], part("so", lo, n), me("so") + [("nxr", C * t, C * t + C)], [(row, c + lo, c + lo + n)], n)
+            gather(T.pvh[:, lo:lo + n], T.sr[:], part("pvo", lo, n), [("pvo", 24 * t + lo // 16, 24 * t + (lo + n) // 16)] + full("sr"), [("pvh", lo, lo + n)], n)
+        list16("nxl", t + 1, "scn", row, c, "e" if t < R - 1 else "h", TS)
+        list16("pvo", t + 1, "scp", "pvh", 0, "h", TS)
 
     def planes(lo, hi):
         return [("win0.%d" % b, lo, hi) for b in range(4)]
@@ -348,50 +365,63 @@ def calls_of(core, rank, T, topo):
             (T.ut[:], T.u[:], full("ut"), 1024)):
         move(out, src, (), key, size)
 
-    iota(T.pi[:], [[0, 1]], 0, 1, full("pi"), 1, small=False)
-    iota(T.t4[:], [[1, 4]], 0, 0, full("t4"), 4)
-    iota(T.jm16[:], [[0, H // 16], [1, 16]], 0, 0, full("jm16"), H)
-    iota(T.J[:, 0:MID], [[1, MID]], 0, 0, [("J", 0, MID)], MID)
-    op("s", lambda e, q: e.activation(T.J[:, MID:WIN], T.J[:, 0:MID], ACT.Copy, bias=float(MID)), [("J", 0, MID)], [("J", MID, WIN)], ("e", MID))
-    iota(T.jo[:], [[0, R], [16, 24]], 0, 0, full("jo"), 72)
+    part = WIN // 4
+    iota(T.J0[:], [[2, part]], 2 * WIN + 1, 0, full("J0"), part)
+    iota(T.pf[:], [[2 * WIN + 18, 2]], -15, 2, full("pf"), 2)
+    for lo in range(0, WIN, part):
+        affine(T.J[:, lo:lo + part], T.J0[:], 0.5 / UNIT, (lo - 0.5) / UNIT, full("J0"), [("J", lo, lo + part)], part)
+    iota(T.jm[:], [[0, H // 16], [2, 16]], -16, 0, full("jm"), H)
+    iota(T.jo[:], [[0, R], [16, 24]], 15, 0, full("jo"), 72)
     iota(T.uo[:], [[16, 8]], 0, 0, full("uo"), 8, small=False)
-    iota(T.sr[:, C:WIN], [[1, G]], C - MID, 0, [("sr", C, WIN)], G)
-    for t in range(R):
-        iota(T["h%d" % t][:, 4 * G:8 * A], [[0, 8 * A - 4 * G]], 0, 0, [("h%d.%d" % (t, b), G, 2 * A) for b in range(4)], 8 * A - 4 * G)
-    iota(T.e4[:], [[0, 1]], -4, -4, full("e4"), 1)
-    op("s", lambda e, q: e.activation(T.ab[:], T.J[:, 0:528], ACT.Abs, bias=T.e4[:, 0:1]), full("J", "e4"), full("ab"), ("e", 528))
-    op("s", lambda e, q: e.activation(T.ee[:], T.ab[:], ACT.Relu, bias=1.0, scale=-1.0), full("ab"), full("ee"), ("e", 528))
+    iota(T.zz[:], [[int(2 * UNIT), 2], [-int(4 * UNIT), 16]], 0, 0, full("zz"), 32)
+    op("g", lambda e, q: e.affine_select(T.sr[:, C:WIN], T.J[:, C:WIN], [[0, G]], AluOpType.is_ge, 0.0, 0, 0), [("J", C, WIN)], [("sr", C, WIN)], ("asel", G))
+    op("v", lambda e, q: e.memset(T.ee[:], 0.0), (), full("ee"), ("h", 516))
+    ts(T.ee[:, 0:516:4], T.J0[:, 0:129], T.pf[:, 1:2], None, AluOpType.is_equal, None, full("J0", "pf", "ee"), full("ee"), 129)
     for b in range(4):
         quant("eq", "es", 128 * b, 128 * b + 128, "ee", 4 - b, 516 - b, full("ee"))
-    ts(T.qi[:], T.pi[:], 15, None, AND, None, full("pi"), full("qi"))
-    copy(lambda: T.qf[:], lambda: T.qi[:], full("qi"), full("qf"), 1, "v")
-    affine("q1", "qf", 1.0, 1.0)
-    ts(T.k16[:], T.qf[:], 15.0, float(S16), LT, MUL, full("qf"), full("k16"))
-    affine("k16p", "k16", 1.0, -float(MID))
-    ts(T.kq4[:], T.t4[:], -0.25, T.k16[:, 0:1], MUL, ADD, full("t4", "k16"), full("kq4"))
-    ts(T.ca[:, 0:H], T.jm16[:], T.q1[:, 0:1], float(S16), EQ, MUL, full("jm16", "q1"), [("ca", 0, H)], H, "h")
-    ts(T.ca[:, H:C], T.jm16[:], T.qf[:, 0:1], -float(K16), EQ, MUL, full("jm16", "qf"), [("ca", H, C)], H, "h")
-    tt(T.c16[:], T.ca[:, 0:H], T.ca[:, H:C], ADD, full("ca"), full("c16"), ("tt", H))
+
+    def column(out, a, s, b, k=0):
+        affine(T[out][:], T[a][:, k:k + 1], s, b if isinstance(b, float) else T[b][:, 0:1], full(a) + ([] if isinstance(b, float) else full(b)), full(out), 1)
+    column("qa", "pf", 1 / 32, BIG)
+    column("qb", "qa", 32.0, -32 * BIG)
+    column("q2", "pf", -1.0, "qb")
+    column("oa", "pf", 1 / 4, BIG, 1)
+    column("ob", "oa", -4.0, 4 * BIG)
+    column("odd", "pf", 1.0, "ob", 1)
+    op("s", lambda e, q: e.activation(T.sg[:], T.jm[:], ACT.Sign, bias=T.q2[:, 0:1]), full("jm", "q2"), full("sg"), ("e", H))
+    affine(T.cm[:, 0:H], T.sg[:], 1.0, 1.0, full("sg"), [("cm", 0, H)], H, "h")
+    for lo in (H, H + H // 2):
+        affine(T.cm[:, lo:lo + H // 2], T.sg[:, 0:H:2], 1.0, 1.0, full("sg"), [("cm", lo, lo + H // 2)], H // 2, "h")
+    affine(T.ca[:], T.sg[:], 32.5, -31.5, full("sg"), full("ca"), H, "h")
+    affine(T.hh[:], T.cm[:, H - 16:H + 8], -0.25, 1.0, [("cm", H - 16, H + 8)], full("hh"), 24)
+    op("v", lambda e, q: e.tensor_tensor_scan(T.mu[:], T.hh[:], T.zz[:, 0:24], UNIT, MUL, MAX), full("hh", "zz"), full("mu"), ("e", 24))
+    affine(T.m4[:], T.mu[:, 23:24], 2.0, 0.0, full("mu"), full("m4"), 1)
+    column("b4", "odd", 1.0, 1.0 - 4 * WIN)
+    column("k16", "q2", -0.5, -7.5)
 
     copy(lambda: T.nxo[:], lambda: T.nxi[:], full("nxi"), full("nxo"), 36, "v")
     op("v", lambda e, q: e.tensor_copy(T.pvr[:].indirect(T.nxo[:]), T.J[:]), full("J", "nxo"), full("pvr"), ("scatter", WIN))
-    for lo in (0, H, C):
-        gather(T.nxr[:, lo:lo + H], T.J[:], T.nxo[:, lo // 16:(lo + H) // 16], full("J", "nxo"), [("nxr", lo, lo + H)], H)
+    for lo, n in runs(ROW_PIECES):
+        gather(T.nxr[:, lo:lo + n], T.J[:], T.nxo[:, lo // 16:(lo + n) // 16], full("J", "nxo"), [("nxr", lo, lo + n)], n)
+    affine(T.nlr[:, C:WIN], T.J[:].indirect(T.nxo[:, 24:36]), UNIT, -float(WIN), full("J", "nxo"), [("nlr", C, WIN)], G, "g")
     for b in range(4):
         ts(T.nx4[:, 24 * b:24 * b + 24], T.nxi[:, 0:24], 4.0, float(b), MUL, ADD, full("nxi"), [("nx4", 24 * b, 24 * b + 24)])
     for lo in (0, H):
-        scan("scp", "pvr", 0, lo, "c16", "e")
-    for b in range(4):
-        ts(T.pv4[:, 24 * b:24 * b + 24], T.scp[:, 15:C:16], T.kq4[:, b:b + 1], 4.0, SUB, MUL, full("scp", "kq4"), [("pv4", 24 * b, 24 * b + 24)])
-    ts(T.pvo[:, 0:24], T.scp[:, 15:C:16], T.k16[:, 0:1], None, SUB, None, full("scp", "k16"), [("pvo", 0, 24)])
-    ts(T.joq[:], T.jo[:], T.qf[:, 0:1], None, ADD, None, full("jo", "qf"), full("joq"), 72)
+        scan("sch", "pvr", 0, lo, ("cm", H), MUL, "e")
+        ts(T.pva[:, lo // 8:(lo + H) // 8], T.sch[:, lo + 7:lo + H:8], T.m4[:, 0:1], T.b4[:, 0:1], MUL, ADD, [("sch", lo, lo + H)] + full("m4", "b4"),
+           [("pva", lo // 8, (lo + H) // 8)])
+    for u in (0, 24):
+        ts(T.pvb[:, u:u + 24], T.pva[:, u:u + 24], 1.0, None, ADD, None, [("pva", u, u + 24)], [("pvb", u, u + 24)])
+    copy(lambda: T.pvf[:], lambda: T.pvr[:, 0:C], full("pvr"), full("pvf"), C)
+    list16("pvo", 0, "scp", "pvf", 0, "h", (C,))
+    affine(T.joq[:], T.jo[:], 1.0, T.k16[:, 0:1], full("jo", "k16"), full("joq"), 72)
     tt(T.lof[:], T.pri[:], T.joq[:], MIN, full("pri", "joq"), full("lof"), ("tt", 72))
     copy(lambda: T.loo[:], lambda: T.lof[:], full("lof"), full("loo"), 72, "v")
     tt(T.hif[:], T.pri[:], T.joq[:], MAX, full("pri", "joq"), full("hif"), ("tt", 72))
     copy(lambda: T.hio[:], lambda: T.hif[:], full("hif"), full("hio"), 72, "v")
     tt(T.dpr[:], T.pri[:], T.joq[:], SUB, full("pri", "joq"), full("dpr"), ("tt", 72))
-    times(T.kd[:], T.dpr[:], "k16", full("dpr"), full("kd"), 72)
-    tt(T.base[:], T.joq[:], T.kd[:], SUB, full("joq", "kd"), full("base"), ("tt", 72))
+    affine(T.kd[:], T.dpr[:], T.k16[:, 0:1], 0.0, full("dpr", "k16"), full("kd"), 72)
+    tt(T.base[:], T.joq[:], T.kd[:], ADD, full("joq", "kd"), full("base"), ("tt", 72))
     quant("uq", "us", 0, 128, "ut", 0, 512, full("ut"))
     copy(lambda: T.uof[:], lambda: T.uo[:], full("uo"), full("uof"), 8, "v")
     op("v", lambda e, q: e.tensor_copy(T.uq16[:, 0:128].bitcast(dt.uint32), T.uq[:, 0:128].bitcast(dt.uint32).indirect(T.uof[:, 0:8])),
@@ -400,39 +430,34 @@ def calls_of(core, rank, T, topo):
 
     sent = [0]
     for t in range(R):
-        read(t, 0, FIRST_PIECES)
-        quant_z(t, 0, A)
-        layer(t, 0, A, 0, A, "h", 0, A)
-        s1 = send(t, False)
-        quant_z(t, G - A, A)
-        layer(t, G - A, G, A, B, "h", A, A)
-        arrival(t, [s1, send(t, True)])
-        scores(t, 0)
-        read(t, H, REST_PIECES)
-        quant_z(t, H, C - H)
-        scores(t, H)
+        read(t)
+        calls = []
+        for lo in range(0, C, A):
+            quant_z(t, lo, A)
+            layer(t, lo, A)
+            if lo < G:
+                calls.append(send(t, lo > 0))
+        arrival(t, calls)
+        for lo, n in runs(SCORES):
+            scores(t, lo, n)
         swap_links(t)
-        layer(t, H, C, H, C - H, "k", 0, C - H)
-        unpack(t + 1, 0, "hq%d" % t, "hs%d" % t, H)
-        unpack(t + 1, H, "kq%d" % t, "ks%d" % t, C - H)
-        unpack(t + 1, C, "gq%d" % t, "gs%d" % t, G)
+        for lo, n in runs(UNPACKS):
+            unpack(t + 1, lo, "hq%d" % t, "hs%d" % t, lo, n)
+        unpack(t + 1, C, "gq%d" % t, "gs%d" % t, 0, G)
     move(T.vt[:], T.v[:], [("so", 0, 1)], full("vt"), 1024)
     quant("vq", "vs", 0, 128, "vt", 0, 512, full("vt"))
-    c = nxrow(R)
-    move(T.nl[:, C:WIN], T.nxr[0:128:16, C:WIN], [("nxr", C, WIN)], [("nl", C, WIN)], 64)
-    move(T.nl[:, 0:C], T.nxr[0:128:16, c:c + C], [("nxr", c, c + C)], [("nl", 0, C)], 128)
+    affine(T.nlr[:, 0:C], T.nxh[:], UNIT, -float(WIN), full("nxh"), [("nlr", 0, C)], C)
+    move(T.nl[:, :], T.nlr[0:128:16, :], full("nlr"), full("nl"), 4 * WIN, rows=8)
     zq, zs, qn = T["zq%d" % R], T["zs%d" % R], "zq%d" % R
-    read(R, 0, LAST_PIECES)
-    lo = 0
-    for n in LAST_TILES:
+    read(R)
+    for lo, n in runs(LAST_TILES):
         quant_z(R, lo, n)
         m = mm("vq", "vs", 0, qn, "zs%d" % R, lo, lo + n)
         move(T.oc[:, 4 * lo:4 * (lo + n)], zq[:, lo:lo + n].bitcast(dt.uint8), [(qn, lo, lo + n)], [("oc", lo, lo + n)], 4 * n)
         copy(lambda lo=lo, n=n: T.y_sb[:, lo:lo + n], m["view"], m["key"], [("y_sb", lo, lo + n)], n)
         move(T.y[:, lo:lo + n], T.y_sb[:, lo:lo + n], [("y_sb", lo, lo + n)], [("y", lo, lo + n)], 4 * n)
-        lo += n
     for k in range(4):
-        move(T.osc[4 * k:4 * k + 4, :], zs[32 * k:32 * k + 4, :], [(qn, 0, C)], [("osc", k, k + 1)], 64, q="s")
+        move(T.osc[4 * k:4 * k + 4, :], zs[32 * k:32 * k + 4, :], [(qn, 0, C)], [("osc", k, k + 1)], 96, q="s", rows=16)
     op("y", None, [("oc", 0, C), ("y", 0, C), ("osc", 0, 4), ("nl", 0, WIN)], (), ("end", 0))
     return ops, sent[0]
 

from concourse.bass import DstId, RemoteDMATransfer
from concourse.mybir import dt, AluOpType, ActivationFunctionType

C, G, R, WIN = 384, 192, 3, 576
H, A, B = G, 128, 64
UNIT = 1024.0
BIG = 4096.0 * 3072.0
F8, BF, F16, F32, I32, U16, U8 = "float8_e4m3fn_x4", "bfloat16", "float16", "float32", "int32", "uint16", "uint8"
PIECES, SCORES, UNPACKS, LAST_TILES = (128, 128, 128), (256, 128), (256, 128), (128, 128, 128)
PAIR_PIECES, LINK_PIECES, ROW_PIECES, TS = (192, 192), (192, 192), (192, 192), (192, 192)
PP = {}
PLAN = """
0 8 7 18 19 24 27 25 28 13 15 9 -10 26 11 29 2 1 23 21 20 14 16 68 22 4 6 3 5 12 30 17 38 39 32 31 59 34 -33 35 40 45 46 47 41 36
48 80 72 37 49 51 71 50 52 53 73 81 75 74 84 83 77 86 87 78 82 54 67 89 96 90 94 92 97 91 76 85 88 100 95 93 107 101 70 42 105
103 98 108 69 79 99 102 106 122 60 111 104 55 109 124 118 64 61 123 110 125 65 119 112 62 56 -113 63 66 116 114 151 155 126 128
149 153 127 129 130 117 152 156 44 43 131 57 132 -115 133 58 134 120 -135 159 163 157 161 389 -139 154 150 136 137 160 164 140
-138 142 145 141 146 144 121 143 165 167 147 148 169 162 158 166 171 168 -173 170 -179 172 185 174 180 191 186 175 181 193 192
176 187 183 182 197 194 188 184 198 200 204 202 177 189 195 199 201 205 203 208 178 190 196 211 215 209 213 206 230 212 216 210
219 214 207 232 231 390 217 224 233 218 -236 225 237 222 226 220 223 234 227 263 221 264 235 257 261 259 258 262 260 239 238 228
240 241 267 268 242 271 265 272 266 269 -244 -247 243 245 -270 246 250 249 248 252 253 254 251 255 256 229 275 273 276 277 274
279 278 281 -287 -289 280 288 293 299 283 290 282 294 300 301 295 285 284 305 302 296 286 306 308 312 310 316 291 297 303 307 309
313 311 292 298 304 317 319 321 323 318 320 314 322 327 338 324 315 325 339 326 340 341 334 328 -344 332 367 330 365 -333 371 369
335 342 329 368 331 345 343 347 346 336 348 349 350 373 377 379 366 372 370 374 -351 -353 375 378 380 376 352 355 -356 354 391
357 358 362 359 361 360 364 363 337 383 384 381 382 -399 -397 392 385 387 386 393 388 400 405 398 394 411 406 412 403 404 409 415
407 417 418 410 395 401 420 413 416 419 408 427 396 402 414 428 421 429 430 422 423 431 424 432 435 434 -425 426 433 436
""".split()
ORDER = [abs(int(k)) for k in PLAN]
ON_VECTOR = [-int(k) for k in PLAN if k[0] == "-"]

SCRATCH = {n: ("sbuf", [128, w], d) for n, w, d in (
    ("nxi", 36, I32), ("pri", 72, I32), ("win0", 4 * WIN, BF), ("ut", 512, BF), ("vt", 512, BF), ("wq", 512, F8), ("wsc", 512, U8),
    ("J0", WIN // 4, F32), ("J", WIN, F32), ("pf", 2, F32), ("qa", 1, F32), ("qb", 1, F32), ("q2", 1, F32),
    ("oa", 1, F32), ("ob", 1, F32), ("odd", 1, F32), ("jm", H, BF), ("sg", H, BF),
    ("cm", 2 * H, F16), ("ca", H, F16), ("hh", 24, F32), ("zz", 32, F32), ("mu", 24, F32),
    ("m4", 1, F32), ("b4", 1, F32), ("k16", 1, F32),
    ("jo", 72, F32), ("joq", 72, F32), ("uo", 8, I32), ("uof", 8, U16),
    ("ee", 516, BF), ("eq", 512, F8), ("es", 512, U8),
    ("uq", 128, F8), ("us", 128, U8), ("uq16", 128, F8), ("us16", 128, U8), ("vq", 128, F8), ("vs", 128, U8),
    ("nxo", 36, U16), ("nx4", 96, U16), ("pva", 48, U16), ("pvb", 48, U16), ("pvo", 96, U16), ("nxl", 96, U16),
    ("so", 72, U16), ("loo", 72, U16), ("hio", 72, U16),
    ("dpr", 72, F32), ("kd", 72, F32), ("base", 72, F32), ("lof", 72, F32), ("hif", 72, F32), ("ta", 72, F32), ("tb", 72, F32),
    ("nxr", 3 * C, F32), ("nxh", C, F16), ("nlr", WIN, F32), ("pvr", WIN, F32), ("sr", WIN, F32), ("pvh", C, F16), ("pvf", C, F16),
    ("S", C, F32), ("SL", C, F32), ("sw", C, F16),
    ("scn", C, F16), ("scp", C, F16), ("sch", C, F16), ("scs", C, F16), ("y_sb", C, F32),
    ("P0", 4 * C, BF), ("P1", 4 * C, BF), ("h", 4 * C, BF))}
for _t in range(R + 1):
    SCRATCH.update({"%s%d" % (n, _t): ("sbuf", [128, w], d) for n, w, d in (("z", 4 * C, BF), ("zq", C, F8), ("zs", C, U8))})
    if _t < R:
        SCRATCH["win%d" % (_t + 1)] = ("sbuf", [128, 4 * WIN], BF)
        SCRATCH.update({"%s%d" % (n, _t): ("sbuf", [128, w], d) for n, w, d in (
            ("hq", C, F8), ("hs", C, U8), ("ra", B, F8), ("rb", B, F8), ("rs", 4 * B, U8), ("gq", G, F8), ("gs", G, U8))})
for _b in range(8):
    SCRATCH["pb%d" % _b] = ("psum", [128, 512], F32)

SEMAPHORES = (["c%d" % i for i in range(70)] + ["d%d" % i for i in range(30)]
              + ["%s%d" % (n, t) for n in ("arra", "arrb", "garr") for t in range(R)] + ["sent"])


def mask_of(engines):
    m = 0
    for e in engines:
        m |= 1 << e
    return m


def relays_of(core, dest, topo):
    c = [k for k in topo.cores_of(core) if k != core and topo.may_write(k, dest)]
    return [[k for k in c if topo.die(k) == topo.die(core)][0], [k for k in c if topo.die(k) != topo.die(core)][0]]


def plan(t, second):
    return [(0, A, B), (1, None, G)] if second else [(0, 0, A // 2), (1, A // 2, A // 2)]


def hop_engines(core, relays, transfers, topo):
    return [topo.engines(core, relays[k])[i::len(transfers)] for i, (k, lo, n) in enumerate(transfers)]


def relay_program(g, core, T, topo):
    mine = [c for c in T.cores if c in topo.cores_of(core)]
    if not mine:
        return
    src = mine[0]
    r = T.rank_of(src)
    total = 0
    for t in range(R):
        dest = T.cores[r ^ (1 << t)]
        rel = relays_of(src, dest, topo)
        for second in (False, True):
            transfers = plan(t, second)
            for (k, lo, n), en in zip(transfers, hop_engines(src, rel, transfers, topo)):
                if rel[k] != core:
                    continue
                rid, pid = topo.addr(dest, core)
                if lo is None:
                    out, inn = T["gs%d" % t][:, 0:n], T["rs%d" % t][:, 0:n]
                else:
                    out, inn = T["gq%d" % t][:, lo:lo + n].bitcast(dt.uint8), T[("rb%d" if second else "ra%d") % t][:, 0:n].bitcast(dt.uint8)
                g.wait_ge(T.sem[("arrb%d" if second else "arra%d") % t], len(en))
                g.remote_dma(out, inn, T.sem["garr%d" % t], T.sem["sent"], pid, rid, topo.mask(core, dest))
                total += len(topo.engines(core, dest))
    if total:
        g.wait_ge(T.sem["sent"], total)


def dependencies(ops):
    hist, out = {}, []
    for i, o in enumerate(ops):
        deps = set(o.get("after", ()))
        for k, lo, hi in o["r"]:
            deps |= {j for (a, b, j, wr) in hist.get(k, ()) if wr and a < hi and lo < b}
        for k, lo, hi in o["w"]:
            deps |= {j for (a, b, j, wr) in hist.get(k, ()) if a < hi and lo < b}
        for k, lo, hi in o["w"]:
            lst = hist.setdefault(k, [])
            lst[:] = [e for e in lst if not (lo <= e[0] and e[1] <= hi)]
            lst.append((lo, hi, i, True))
        for k, lo, hi in o["r"]:
            hist.setdefault(k, []).append((lo, hi, i, False))
        deps.discard(i)
        out.append(deps)
    return out


def arrange(ops):
    order = ORDER or list(range(len(ops)))
    at = {k: i for i, k in enumerate(order)}
    assert sorted(at) == list(range(len(ops)))
    assert all(at[j] < at[i] for i, d in enumerate(dependencies(ops)) for j in d)
    assert all(ops[i]["q"] == "vs" for i in ON_VECTOR)
    readers = {}
    for i, o in enumerate(ops):
        if o["q"] == "vs":
            o["q"] = "v" if i in ON_VECTOR else "s"
        for k, lo, hi in o["r"]:
            if k[0] == "@":
                readers.setdefault(k, set()).add(i)
    free, names = ["pb%d" % b for b in range(8)], {}
    for i in order:
        o = ops[i]
        if "m" in o:
            names[o["w"][0][0]] = o["m"]["k"] = free.pop(0)
        for k, lo, hi in o["r"]:
            if k[0] == "@":
                readers[k].discard(i)
                if not readers[k]:
                    free.append(names[k])
    for o in ops:
        o["after"] = ()
        for a in "rw":
            o[a] = [(names.get(k, k), lo, hi) for k, lo, hi in o[a]]
    return [ops[i] for i in order]


def emit(g, T, ops):
    queues = {"g": g, "v": g.vector, "s": g.scalar, "p": g.tensor, "y": g.sync}
    know, at, need, used = {q: set() for q in queues}, [], [], set()
    for i, (o, deps) in enumerate(zip(ops, dependencies(ops))):
        w = []
        if o["q"] is None:
            at.append(set())
        else:
            kq = know[o["q"]]
            for j in sorted(deps, reverse=True):
                if j not in kq:
                    w.append(j)
                    used.add(j)
                    kq.add(j)
                    kq |= at[j]
            at.append(set(kq))
        need.append(w)
    last, count, sem = {}, {}, {}
    for i, o in enumerate(ops):
        if i not in used:
            continue
        if o["q"] is None:
            sem[i] = (o["sem"], o["val"])
            continue
        kind, n = ("d", 16) if o["c"][0] == "dma" else ("c", 1)
        k = 0
        while (kind, k) in last and last[(kind, k)] not in at[i]:
            k += 1
        last[(kind, k)] = i
        count[(kind, k)] = count.get((kind, k), 0) + n
        sem[i] = ("%s%d" % (kind, k), count[(kind, k)])
    for i, o in enumerate(ops):
        if o["q"] is None:
            continue
        e = queues[o["q"]]
        for j in need[i]:
            e.wait_ge(T.sem[sem[j][0]], sem[j][1])
        if o["f"] is None:
            continue
        ins = o["f"](e, o["q"])
        if i in sem:
            ins.then_inc(T.sem[sem[i][0]], 16 if o["c"][0] == "dma" else 1)


def calls_of(core, rank, T, topo):
    ops = []
    ADD, SUB, MUL, MAX, MIN = AluOpType.add, AluOpType.subtract, AluOpType.mult, AluOpType.max, AluOpType.min
    GT = AluOpType.is_gt
    ACT = ActivationFunctionType

    def op(q, f, r, w, c, **kw):
        ops.append(dict(q=q, f=f, r=list(r), w=list(w), c=c, **kw))
        return len(ops) - 1

    def full(*names):
        return [(n, 0, 1 << 20) for n in names]

    def runs(pieces, lo=0):
        out = []
        for n in pieces:
            out.append((lo, n))
            lo += n
        return out

    def move(out, src, r, w, size, q="y", rows=128):
        op(q, lambda e, q: e.dma_start(out, src), r, w, ("dma", size, rows))

    def copy(out, in_, r, w, n, q="vs"):
        op(q, lambda e, q: e.tensor_copy(out(), in_()) if q == "v" else e.activation(out(), in_(), ACT.Copy), r, w, ("e", n))

    def gather(out, win, off, r, w, n):
        op("vs", lambda e, q: e.tensor_copy(out, win.indirect(off)) if q == "v" else e.activation(out, win.indirect(off), ACT.Copy), r, w, ("g", n))

    def tt(out, a, b, o, r, w, c):
        op("v", lambda e, q: e.tensor_tensor(out, a, b, o), r, w, c)

    def ts(out, a, s1, s2, o1, o2, r, w, n=64, kind="e"):
        if o2 is None:
            op("v", lambda e, q: e.tensor_scalar(out, a, s1, None, o1), r, w, (kind, n))
        else:
            op("v", lambda e, q: e.tensor_scalar(out, a, s1, s2, o1, o2), r, w, (kind, n))

    def affine(out, a, s, b, r, w, n, kind="e"):
        func = ACT.Copy if isinstance(s, float) and isinstance(b, float) else ACT.Identity
        op("vs", lambda e, q: e.tensor_scalar(out, a, s, b, MUL, ADD) if q == "v" else e.activation(out, a, func, scale=s, bias=b), r, w, (kind, n))

    def iota(out, pat, base, cm, w, n, small=True):
        if small:
            op("g", lambda e, q: e.iota(out, pat, base, cm, allow_small_or_imprecise_dtypes=True), (), w, ("iota", n))
        else:
            op("g", lambda e, q: e.iota(out, pat, base, cm), (), w, ("iota", n))

    def quant(qn, sn, a, b, src, lo, hi, r):
        op("v", lambda e, q: e.quantize_mx(T[qn][:, a:b], T[sn][:, a:b], T[src][:, lo:hi]), r, [(qn, a, b)], ("q", hi - lo))

    made = [0]

    def mm(wn, wsn, wa, xn, xsn, a, b):
        made[0] += 1
        m = {"key": full("@%d" % made[0])}
        op("p", lambda e, q: e.matmul_mx(T[m["k"]][:, 0:b - a], T[wn][:, wa:wa + 128], T[wsn][:, wa:wa + 128], T[xn][:, a:b], T[xsn][:, a:b], True, True),
           [(wn, wa, wa + 128), (wsn + ".load", 0, 1), (xn, a, b)], m["key"], ("mm", b - a), m=m)
        m["view"] = lambda: T[m["k"]][:, 0:b - a]
        return m

    def first_read():
        for h in range(2):
            for lo, n in runs(PP.get((0, h), PIECES)):
                keys = [("win0.%d" % b, 0, WIN) for b in (h, h + 2)]
                pk = [("P0.%d" % b, lo, lo + n) for b in (h, h + 2)]
                a, l2, u = 2 * C * h + 2 * lo, ("pva", "pvb")[h], lo // 8
                for i in range(2):
                    c = 24 * (h + 2 * i) + lo // 16
                    gather(T.P0[:, a + i:a + 2 * n:2], T.win0[:], T.nx4[:, c:c + n // 16], [keys[i], ("nx4", c, c + n // 16)], [pk[i]], n)
                tt(T.z0[:, 4 * lo + h:4 * (lo + n):2], T.win0[:].indirect(T[l2][:, u:u + n // 8]), T.P0[:, a:a + 2 * n], ADD,
                   keys + pk + [(l2, u, u + n // 8)], [("z0.%d" % b, lo, lo + n) for b in (h, h + 2)], ("g", 2 * n))

    def read(t):
        if t == 0:
            return first_read()
        for b in range(4):
            for lo, n in runs(PP.get((t, b), PIECES)):
                win, u, key, pk = T["win%d" % t][:, WIN * b:WIN * b + WIN], 24 * t + lo // 16, ("win%d.%d" % (t, b), 0, WIN), ("P%d.%d" % (t % 2, b), lo, lo + n)
                P = T["P%d" % (t % 2)][:, C * b + lo:C * b + lo + n]
                gather(P, win, T.nxl[:, u:u + n // 16], [key, ("nxl", u, u + n // 16)], [pk], n)
                tt(T["z%d" % t][:, 4 * lo + b:4 * (lo + n):4], win.indirect(T.pvo[:, u:u + n // 16]), P, ADD, [key, pk, ("pvo", u, u + n // 16)],
                   [("z%d.%d" % (t, b), lo, lo + n)], ("g", n))

    def quant_z(t, lo, n):
        quant("zq%d" % t, "zs%d" % t, lo, lo + n, "z%d" % t, 4 * lo, 4 * (lo + n), [("z%d.%d" % (t, b), lo, lo + n) for b in range(4)])

    def layer(t, lo, n):
        for b in range(4):
            m, out = mm("wq", "wsc", 128 * b, "zq%d" % t, "zs%d" % t, lo, lo + n), T.h[:, 4 * lo + b:4 * (lo + n):4]
            op("vs", lambda e, q, m=m, out=out: e.activation(out, m["view"](), ACT.Relu, scale=0.015625) if q == "s" else
               e.tensor_scalar(out, m["view"](), 0.0, 0.015625, MAX, MUL), m["key"], [("h.%d" % b, lo, lo + n)], ("e", n))
        quant("hq%d" % t, "hs%d" % t, lo, lo + n, "h", 4 * lo, 4 * (lo + n), [("h.%d" % b, lo, lo + n) for b in range(4)])

    def unpack(t, at, qn, sn, lo, n):
        for b in range(4):
            m = mm("eq", "es", 128 * b, qn, sn, lo, lo + n)
            copy(lambda a=WIN * b + at: T["win%d" % t][:, a:a + n], m["view"], m["key"], [("win%d.%d" % (t, b), at, at + n)], n)

    def send(t, second):
        dest = T.cores[rank ^ (1 << t)]
        rel = relays_of(core, dest, topo)
        transfers = plan(t, second)
        en = hop_engines(core, rel, transfers, topo)
        ids = [topo.addr(rel[k], core) for k, lo, n in transfers]
        land = T[("rb%d" if second else "ra%d") % t]
        sides = [(T["hs%d" % t][:, 0:2 * A], T["rs%d" % t][:, :]) if lo is None else
                 (T["hq%d" % t][:, lo:lo + n].bitcast(dt.uint8), land[:, 0:n].bitcast(dt.uint8)) for k, lo, n in transfers]
        sem = T.sem[("arrb%d" if second else "arra%d") % t]
        i = op("g", lambda e, q: e.remote_dma_fused(
            [RemoteDMATransfer(dst_ids=[DstId(rid=ids[k][0], pnc=ids[k][1])], dma_engine_mask=mask_of(en[k]), remote_sem=sem,
                               src=sides[k][0], dst=sides[k][1]) for k in range(len(transfers))], local_sem=T.sem["sent"]),
            [("hq%d" % t, 0, 2 * A if second else A)], (), ("send", t, second))
        sent[0] += sum(len(x) for x in en)
        return i

    def arrival(t, calls):
        rel = relays_of(T.cores[rank ^ (1 << t)], core, topo)
        op(None, None, (), full("gq%d" % t), ("arrive", t), sem="garr%d" % t, after=calls,
           val=sum(len(topo.engines(rel[k], core)) for k, lo, n in plan(t, False) + plan(t, True)))

    def scan(dst, src, a, lo, c, o, kind):
        op("v", lambda e, q: e.tensor_tensor_scan(T[dst][:, lo:lo + H], T[c[0]][:, c[1]:c[1] + H], T[src][:, a + lo:a + lo + H], 0.0, o, MAX),
           [(src, a + lo, a + lo + H), (c[0], c[1], c[1] + H)], [(dst, lo, lo + H)], (kind, H))

    def list16(dst, t, sc, src, a, kind, pieces):
        for lo in (0, H):
            scan(sc, src, a, lo, ("cm", 0), MUL, kind)
        for lo, n in runs(pieces):
            u = 24 * t + lo // 16
            ts(T[dst][:, u:u + n // 16], T[sc][:, lo + 15:lo + n:16], T.mu[:, 15:16], -float(WIN), MUL, ADD, [(sc, lo, lo + n)] + full("mu"), [(dst, u, u + n // 16)])

    def scores(t, lo, n):
        m = mm("uq16", "us16", 0, "zq%d" % t, "zs%d" % t, lo, lo + n)
        copy(lambda: T.S[:, lo:lo + n], m["view"], m["key"], [("S", lo, lo + n)], n)

    def swap_links(t):
        a = slice(24 * t, 24 * t + 24)

        def me(*names):
            return [(n, t, t + 1) for n in names]

        def part(name, lo, n):
            return T[name][:, 24 * t + lo // 16:24 * t + (lo + n) // 16]
        for lo, n in runs(PAIR_PIECES):
            gather(T.SL[:, lo:lo + n], T.S[:], part("loo", lo, n), full("S", "loo"), [("SL", lo, lo + n)], n)
            tt(T.sw[:, lo:lo + n], T.S[:].indirect(part("hio", lo, n)), T.SL[:, lo:lo + n], GT, full("S", "hio") + [("SL", lo, lo + n)], [("sw", lo, lo + n)], ("g", n))
        for lo in (0, H):
            scan("scs", "sw", 0, lo, ("ca", 0), ADD, "h")
        tt(T.ta[:, a], T.scs[:, 15:C:16], T.dpr[:, a], MUL, full("scs", "dpr"), me("ta"), ("tt", 24))
        tt(T.tb[:, a], T.ta[:, a], T.base[:, a], ADD, me("ta") + full("base"), me("tb"), ("tt", 24))
        copy(lambda: T.so[:, a], lambda: T.tb[:, a], me("tb"), me("so"), 24, "v")
        for lo, n in runs(ROW_PIECES):
            gather(T.sr[:, lo:lo + n], T.J[:, 0:C], part("so", lo, n), me("so") + full("J"), [("sr", lo, lo + n)], n)
        row, c = ("nxr", C * t + C) if t < R - 1 else ("nxh", 0)
        for lo, n in runs(LINK_PIECES):
            gather(T[row][:, c + lo:c + lo + n], T.nxr[:, C * t:C * t + C], part("so", lo, n), me("so") + [("nxr", C * t, C * t + C)], [(row, c + lo, c + lo + n)], n)
            gather(T.pvh[:, lo:lo + n], T.sr[:], part("pvo", lo, n), [("pvo", 24 * t + lo // 16, 24 * t + (lo + n) // 16)] + full("sr"), [("pvh", lo, lo + n)], n)
        list16("nxl", t + 1, "scn", row, c, "e" if t < R - 1 else "h", TS)
        list16("pvo", t + 1, "scp", "pvh", 0, "h", TS)

    def planes(lo, hi):
        return [("win0.%d" % b, lo, hi) for b in range(4)]
    for out, src, key, size in (
            (T.nxi[:], T.nx[:], full("nxi"), 144), (T.win0[:, 0:4 * C], T.x[:], planes(0, C), 8 * C), (T.win0[:, 4 * C:4 * WIN], T.gh[:], planes(C, WIN), 8 * G),
            (T.wq[:].bitcast(dt.uint8), T.wc[:], full("wq"), 2048), (T.wsc[:], T.ws[:], full("wsc.load"), 512), (T.pri[:], T.pr[:], full("pri"), 288),
            (T.ut[:], T.u[:], full("ut"), 1024)):
        move(out, src, (), key, size)

    part = WIN // 4
    iota(T.J0[:], [[2, part]], 2 * WIN + 1, 0, full("J0"), part)
    iota(T.pf[:], [[2 * WIN + 18, 2]], -15, 2, full("pf"), 2)
    for lo in range(0, WIN, part):
        affine(T.J[:, lo:lo + part], T.J0[:], 0.5 / UNIT, (lo - 0.5) / UNIT, full("J0"), [("J", lo, lo + part)], part)
    iota(T.jm[:], [[0, H // 16], [2, 16]], -16, 0, full("jm"), H)
    iota(T.jo[:], [[0, R], [16, 24]], 15, 0, full("jo"), 72)
    iota(T.uo[:], [[16, 8]], 0, 0, full("uo"), 8, small=False)
    iota(T.zz[:], [[int(2 * UNIT), 2], [-int(4 * UNIT), 16]], 0, 0, full("zz"), 32)
    op("g", lambda e, q: e.affine_select(T.sr[:, C:WIN], T.J[:, C:WIN], [[0, G]], AluOpType.is_ge, 0.0, 0, 0), [("J", C, WIN)], [("sr", C, WIN)], ("asel", G))
    op("v", lambda e, q: e.memset(T.ee[:], 0.0), (), full("ee"), ("h", 516))
    ts(T.ee[:, 0:516:4], T.J0[:, 0:129], T.pf[:, 1:2], None, AluOpType.is_equal, None, full("J0", "pf", "ee"), full("ee"), 129)
    for b in range(4):
        quant("eq", "es", 128 * b, 128 * b + 128, "ee", 4 - b, 516 - b, full("ee"))

    def column(out, a, s, b, k=0):
        affine(T[out][:], T[a][:, k:k + 1], s, b if isinstance(b, float) else T[b][:, 0:1], full(a) + ([] if isinstance(b, float) else full(b)), full(out), 1)
    column("qa", "pf", 1 / 32, BIG)
    column("qb", "qa", 32.0, -32 * BIG)
    column("q2", "pf", -1.0, "qb")
    column("oa", "pf", 1 / 4, BIG, 1)
    column("ob", "oa", -4.0, 4 * BIG)
    column("odd", "pf", 1.0, "ob", 1)
    op("s", lambda e, q: e.activation(T.sg[:], T.jm[:], ACT.Sign, bias=T.q2[:, 0:1]), full("jm", "q2"), full("sg"), ("e", H))
    affine(T.cm[:, 0:H], T.sg[:], 1.0, 1.0, full("sg"), [("cm", 0, H)], H, "h")
    for lo in (H, H + H // 2):
        affine(T.cm[:, lo:lo + H // 2], T.sg[:, 0:H:2], 1.0, 1.0, full("sg"), [("cm", lo, lo + H // 2)], H // 2, "h")
    affine(T.ca[:], T.sg[:], 32.5, -31.5, full("sg"), full("ca"), H, "h")
    affine(T.hh[:], T.cm[:, H - 16:H + 8], -0.25, 1.0, [("cm", H - 16, H + 8)], full("hh"), 24)
    op("v", lambda e, q: e.tensor_tensor_scan(T.mu[:], T.hh[:], T.zz[:, 0:24], UNIT, MUL, MAX), full("hh", "zz"), full("mu"), ("e", 24))
    affine(T.m4[:], T.mu[:, 23:24], 2.0, 0.0, full("mu"), full("m4"), 1)
    column("b4", "odd", 1.0, 1.0 - 4 * WIN)
    column("k16", "q2", -0.5, -7.5)

    copy(lambda: T.nxo[:], lambda: T.nxi[:], full("nxi"), full("nxo"), 36, "v")
    op("v", lambda e, q: e.tensor_copy(T.pvr[:].indirect(T.nxo[:]), T.J[:]), full("J", "nxo"), full("pvr"), ("scatter", WIN))
    for lo, n in runs(ROW_PIECES):
        gather(T.nxr[:, lo:lo + n], T.J[:], T.nxo[:, lo // 16:(lo + n) // 16], full("J", "nxo"), [("nxr", lo, lo + n)], n)
    affine(T.nlr[:, C:WIN], T.J[:].indirect(T.nxo[:, 24:36]), UNIT, -float(WIN), full("J", "nxo"), [("nlr", C, WIN)], G, "g")
    for b in range(4):
        ts(T.nx4[:, 24 * b:24 * b + 24], T.nxi[:, 0:24], 4.0, float(b), MUL, ADD, full("nxi"), [("nx4", 24 * b, 24 * b + 24)])
    for lo in (0, H):
        scan("sch", "pvr", 0, lo, ("cm", H), MUL, "e")
        ts(T.pva[:, lo // 8:(lo + H) // 8], T.sch[:, lo + 7:lo + H:8], T.m4[:, 0:1], T.b4[:, 0:1], MUL, ADD, [("sch", lo, lo + H)] + full("m4", "b4"),
           [("pva", lo // 8, (lo + H) // 8)])
    for u in (0, 24):
        ts(T.pvb[:, u:u + 24], T.pva[:, u:u + 24], 1.0, None, ADD, None, [("pva", u, u + 24)], [("pvb", u, u + 24)])
    copy(lambda: T.pvf[:], lambda: T.pvr[:, 0:C], full("pvr"), full("pvf"), C)
    list16("pvo", 0, "scp", "pvf", 0, "h", (C,))
    affine(T.joq[:], T.jo[:], 1.0, T.k16[:, 0:1], full("jo", "k16"), full("joq"), 72)
    tt(T.lof[:], T.pri[:], T.joq[:], MIN, full("pri", "joq"), full("lof"), ("tt", 72))
    copy(lambda: T.loo[:], lambda: T.lof[:], full("lof"), full("loo"), 72, "v")
    tt(T.hif[:], T.pri[:], T.joq[:], MAX, full("pri", "joq"), full("hif"), ("tt", 72))
    copy(lambda: T.hio[:], lambda: T.hif[:], full("hif"), full("hio"), 72, "v")
    tt(T.dpr[:], T.pri[:], T.joq[:], SUB, full("pri", "joq"), full("dpr"), ("tt", 72))
    affine(T.kd[:], T.dpr[:], T.k16[:, 0:1], 0.0, full("dpr", "k16"), full("kd"), 72)
    tt(T.base[:], T.joq[:], T.kd[:], ADD, full("joq", "kd"), full("base"), ("tt", 72))
    quant("uq", "us", 0, 128, "ut", 0, 512, full("ut"))
    copy(lambda: T.uof[:], lambda: T.uo[:], full("uo"), full("uof"), 8, "v")
    op("v", lambda e, q: e.tensor_copy(T.uq16[:, 0:128].bitcast(dt.uint32), T.uq[:, 0:128].bitcast(dt.uint32).indirect(T.uof[:, 0:8])),
       full("uq", "uof"), full("uq16"), ("g", 128))
    gather(T.us16[:, 0:128], T.us[:, 0:128], T.uof[:, 0:8], full("uq", "uof"), full("us16.load"), 128)

    sent = [0]
    for t in range(R):
        read(t)
        calls = []
        for lo in range(0, C, A):
            quant_z(t, lo, A)
            layer(t, lo, A)
            if lo < G:
                calls.append(send(t, lo > 0))
        arrival(t, calls)
        for lo, n in runs(SCORES):
            scores(t, lo, n)
        swap_links(t)
        for lo, n in runs(UNPACKS):
            unpack(t + 1, lo, "hq%d" % t, "hs%d" % t, lo, n)
        unpack(t + 1, C, "gq%d" % t, "gs%d" % t, 0, G)
    move(T.vt[:], T.v[:], [("so", 0, 1)], full("vt"), 1024)
    quant("vq", "vs", 0, 128, "vt", 0, 512, full("vt"))
    affine(T.nlr[:, 0:C], T.nxh[:], UNIT, -float(WIN), full("nxh"), [("nlr", 0, C)], C)
    move(T.nl[:, :], T.nlr[0:128:16, :], full("nlr"), full("nl"), 4 * WIN, rows=8)
    zq, zs, qn = T["zq%d" % R], T["zs%d" % R], "zq%d" % R
    read(R)
    for lo, n in runs(LAST_TILES):
        quant_z(R, lo, n)
        m = mm("vq", "vs", 0, qn, "zs%d" % R, lo, lo + n)
        move(T.oc[:, 4 * lo:4 * (lo + n)], zq[:, lo:lo + n].bitcast(dt.uint8), [(qn, lo, lo + n)], [("oc", lo, lo + n)], 4 * n)
        copy(lambda lo=lo, n=n: T.y_sb[:, lo:lo + n], m["view"], m["key"], [("y_sb", lo, lo + n)], n)
        move(T.y[:, lo:lo + n], T.y_sb[:, lo:lo + n], [("y_sb", lo, lo + n)], [("y", lo, lo + n)], 4 * n)
    for k in range(4):
        move(T.osc[4 * k:4 * k + 4, :], zs[32 * k:32 * k + 4, :], [(qn, 0, C)], [("osc", k, k + 1)], 96, q="s", rows=16)
    op("y", None, [("oc", 0, C), ("y", 0, C), ("osc", 0, 4), ("nl", 0, WIN)], (), ("end", 0))
    return ops, sent[0]


def rank_program(g, core, T, topo):
    rank = T.rank_of(core)
    if rank is None:
        return relay_program(g, core, T, topo)
    ops, sent = calls_of(core, rank, T, topo)
    emit(g, T, arrange(ops))
    g.wait_ge(T.sem.sent, sent)
